import numpy as np
import ml_dtypes


def mxq(x, axis, fmt="e4m3"):
    dtype, down = {"e4m3": (ml_dtypes.float8_e4m3fn, 7), "e5m2": (ml_dtypes.float8_e5m2, 14)}[fmt]
    v = np.moveaxis(np.asarray(x, np.float32).astype(ml_dtypes.bfloat16).astype(np.float64), axis, -1)
    blocks = v.reshape(v.shape[:-1] + (-1, 32))
    amax = np.abs(blocks).max(-1, keepdims=True)
    byte = np.maximum(np.where(amax > 0, np.frexp(amax)[1] - 1 + 127, 0) - down, 1)
    scale = np.exp2(byte - 127.0)
    codes = (blocks / scale).astype(np.float32).astype(dtype).astype(np.float64)
    return np.moveaxis((codes * scale).reshape(v.shape), -1, axis)


WIDE = False


def mx_kscale(k):
    if not WIDE:
        return np.ones(k)
    levels = np.array([24, -24, 12, -12, 0])
    if k % 512:
        return np.exp2(np.random.permutation(np.resize(levels, k // 32))).repeat(32)
    a = np.empty((k // 512, 16))
    for p in range(k // 512):
        a[p, :8] = np.random.permutation(np.resize(levels, 8))
        for g in range(8):
            far = levels[np.abs(levels - a[p, g]) >= 10]
            a[p, g + 8] = far[np.random.randint(len(far))]
    return np.exp2(a.ravel()).repeat(32)


def f64(x):
    return np.asarray(x).astype(np.float64)


def striped(idx):
    return np.tile(idx.reshape(-1, 16).T, (8, 1)).astype(np.uint16)


def unstriped(offs):
    return offs[:16].T.reshape(-1).astype(np.int64)


E2M1 = np.array([0.0, 0.5, 1.0, 1.5, 2.0, 3.0, 4.0, 6.0, -0.0, -0.5, -1.0, -1.5, -2.0, -3.0, -4.0, -6.0])


def pack_weight(w, fmt):
    k, n = w.shape
    w = f64(np.asarray(w, np.float32).astype(ml_dtypes.bfloat16)).reshape(k // 32, 32, n)
    amax = np.abs(w).max(1)
    if fmt == "e4m3":
        byte = np.frexp(amax)[1] - 1 + 127 - 7
    else:
        mant, ex = np.frexp(amax / 6.0)
        byte = np.where(mant > 0.5, ex, ex - 1) + 127
    byte = np.clip(np.where(amax > 0, byte, 1), 1, 254)
    scaled = (w * np.exp2(127.0 - byte)[:, None, :]).reshape(k, n).astype(np.float32)
    by_word = np.ascontiguousarray(scaled.reshape(k // 512, 128, 4, n).transpose(0, 1, 3, 2))
    if fmt == "e4m3":
        words = by_word.astype(ml_dtypes.float8_e4m3fn).view(np.uint8)
    else:
        c = by_word.astype(ml_dtypes.float4_e2m1fn).view(np.uint8) & 0xF
        words = (c[..., 0::2] | (c[..., 1::2] << 4)).reshape(k // 512, 128, 2 * n)
    return np.ascontiguousarray(words), np.ascontiguousarray(byte.astype(np.uint8).reshape(k // 512, 16, n))


def unpack_weight(words, scales, fmt):
    g, _, n = scales.shape
    words = np.ascontiguousarray(words).reshape(g, 128, n, -1)
    if fmt == "e4m3":
        vals = words.view(ml_dtypes.float8_e4m3fn).astype(np.float64)
    else:
        nib = np.empty((g, 128, n, 4), np.uint8)
        nib[..., 0::2] = words & 0xF
        nib[..., 1::2] = words >> 4
        vals = E2M1[nib]
    vals = vals * np.repeat(np.exp2(scales.astype(np.float64) - 127.0), 8, axis=1)[..., None]
    return vals.transpose(0, 1, 3, 2).reshape(g * 512, n)


def pack_table4(v):
    words, scales = pack_weight(v, "e2m1")
    g, t = words.shape[0] // 2, v.shape[1]
    return np.ascontiguousarray(words.reshape(g, 2, 128, t, 2).transpose(0, 2, 3, 1, 4).reshape(g, 128, t, 4)), scales


def unpack_table4(words, scales):
    g, _, t, _ = words.shape
    return unpack_weight(words.reshape(g, 128, t, 2, 2).transpose(0, 3, 1, 2, 4).reshape(2 * g, 128, 2 * t), scales, "e2m1")


def silu(f):
    return f / (1.0 + np.exp(-np.maximum(f, -700.0)))


def sigm(f):
    return 1.0 / (1.0 + np.exp(-np.maximum(f, -700.0)))


K, L, N, T, J = 512, 1024, 512, 2048, 1024


def setup_inputs():
    n = np.random.standard_normal
    s = mx_kscale(K)[:, None]
    s2 = mx_kscale(L)[:, None]
    p_tab = pack_weight(n((K, T)) * s, "e4m3")
    p_tab2 = pack_table4(n((L, T)) * s2)
    p_zv = pack_weight(n((K, N)) / np.sqrt(K) / s, "e2m1")
    p_zt = pack_weight(n((L, N)) / np.sqrt(L) / s2, "e2m1")
    p_wt = pack_weight(n((L, N)) / np.sqrt(L) / s2, "e4m3")
    return {
        "tab_words": p_tab[0],
        "tab_scales": p_tab[1],
        "tab2_words": p_tab2[0],
        "tab2_scales": p_tab2[1],
        "zv_words": p_zv[0],
        "zv_scales": p_zv[1],
        "zt_words": p_zt[0],
        "zt_scales": p_zt[1],
        "b": (0.3 * n(N)).astype(np.float32),
        "wv": (n((K, N)) / np.sqrt(K) / s).astype(np.float32),
        "wt_words": p_wt[0],
        "wt_scales": p_wt[1],
        "offs": striped(np.random.permutation(T)[:J]),
        "offs2": striped(np.random.permutation(T)[:J]),
    }


def reference(tab_words, tab_scales, tab2_words, tab2_scales, zv_words, zv_scales, zt_words, zt_scales, b, wv, wt_words, wt_scales, offs, offs2):
    idx = unstriped(offs)
    idx2 = unstriped(offs2)
    tab_ = unpack_weight(tab_words, tab_scales, "e4m3")[:, idx]
    tab2_ = unpack_table4(tab2_words, tab2_scales)[:, idx2]
    zv_ = unpack_weight(zv_words, zv_scales, "e2m1")
    zt_ = unpack_weight(zt_words, zt_scales, "e2m1")
    z = zv_.T @ tab_ + zt_.T @ tab2_
    gate = sigm(z + f64(b)[:, None])
    wv_ = mxq(f64(wv), 0, "e4m3")
    wt_ = unpack_weight(wt_words, wt_scales, "e4m3")
    hv = wv_.T @ tab_
    ht = wt_.T @ tab2_
    av = silu(hv)
    at = silu(ht)
    return at + gate * (av - at)

@@ -1,0 +1,149 @@
+from contextlib import ExitStack
+
+import concourse.mybir as mybir
+
+K, L, N, T, J = 512, 1024, 512, 2048, 1024
+FLOPS = 2 * N * J * (2 * K + 2 * L)
+
+F32 = mybir.dt.float32
+BF16 = mybir.dt.bfloat16
+I32 = mybir.dt.int32
+U32 = mybir.dt.uint32
+U16 = mybir.dt.uint16
+U8 = mybir.dt.uint8
+FP8X4 = mybir.dt.float8_e4m3fn_x4
+FP4X4 = mybir.dt.float4_e2m1fn_x4
+ALU = mybir.AluOpType
+ACT = mybir.ActivationFunctionType
+
+P = 128
+PACK = 4
+CHUNK = 512
+QUADS = 4
+
+
+def tile_list_gmu_silu_none_kernel(
+    tc, tab_words, tab_scales, tab2_words, tab2_scales, zv_words, zv_scales, zt_words, zt_scales,
+    b, wv, wt_words, wt_scales, offs, offs2, out,
+):
+    nc = tc.nc
+    with ExitStack() as ctx:
+        keep = ctx.enter_context(tc.tile_pool(name="keep", bufs=1))
+        ring = ctx.enter_context(tc.tile_pool(name="ring", bufs=3))
+        psum = ctx.enter_context(tc.psum_pool(name="psum", bufs=1))
+
+        list1 = keep.tile([P, J // 16], U16, name="list1")
+        list2 = keep.tile([P, J // 16], U16, name="list2")
+        tab_w = keep.tile([P, T], I32, name="tab_w", align_bytes=64)
+        tab2_w = keep.tile([P, T], I32, name="tab2_w", align_bytes=64)
+        tab_s = keep.tile([P, T], U8, name="tab_s", align_bytes=64)
+        tab2_s = keep.tile([P, T], U8, name="tab2_s", align_bytes=64)
+        w_scales = keep.tile([P, 5 * N], U8, name="w_scales", align_bytes=64)
+        wt_w = keep.tile([P, 2, N], I32, name="wt_w", align_bytes=64)
+        zv_w = keep.tile([P, 2 * N], U8, name="zv_w", align_bytes=64)
+        zt_w = keep.tile([P, 2, 2 * N], U8, name="zt_w", align_bytes=64)
+        wv_raw = [keep.tile([P, PACK, N // 2], F32, name="wv_raw%d" % h, align_bytes=64) for h in range(2)]
+        wv_bf = keep.tile([P, N, PACK], BF16, name="wv_bf", align_bytes=64)
+        wv_codes = keep.tile([P, N], U32, name="wv_codes", align_bytes=64)
+        wv_scales = keep.tile([P, N], U8, name="wv_scales", align_bytes=64)
+        b_sb = keep.tile([P, N // P], F32, name="b_sb")
+        half_b = keep.tile([P, N // P], F32, name="half_b")
+        v_s = keep.tile([P, J], U8, name="v_s", align_bytes=64)
+        v2_s0 = keep.tile([P, J], U8, name="v2_s0", align_bytes=64)
+        v2_s1 = keep.tile([P, J], U8, name="v2_s1", align_bytes=64)
+        warm_in = keep.tile([P, 1], F32, name="warm_in")
+        warm_out = keep.tile([P, 1], F32, name="warm_out")
+
+        nc.vector.memset(tab2_s[:].bitcast(I32), 0)
+        nc.vector.memset(tab_s[:].bitcast(I32), 0)
+        nc.vector.memset(warm_in[:], 0.0)
+        nc.vector.memset(w_scales[:].bitcast(I32), 0)
+        nc.vector.memset(v2_s1[:].bitcast(I32), 0)
+        nc.scalar.activation(out=warm_out[:], in_=warm_in[:], func=ACT.Silu)
+
+        wv_rows = wv.rearrange("(p i) n -> p i n", i=PACK)
+        nc.sync.dma_start(list2[:], offs2)
+        nc.sync.dma_start(list1[:], offs)
+        for q in range(QUADS):
+            nc.sync.dma_start(tab2_s[32 * q : 32 * q + 8, :].bitcast(I32), tab2_scales[:, 4 * q : 4 * q + 4, :].bitcast(I32))
+        for h in range(2):
+            nc.sync.dma_start(wv_raw[h][:], wv_rows[:, :, h * (N // 2) : (h + 1) * (N // 2)])
+        for q in range(QUADS):
+            nc.gpsimd.dma_start(tab_s[32 * q : 32 * q + 4, :].bitcast(I32), tab_scales[0, 4 * q : 4 * q + 4, :].bitcast(I32))
+        nc.sync.dma_start(tab_w[:], tab_words[0].rearrange("p t i -> p (t i)").bitcast(I32))
+        staged = w_scales[0:16, :].bitcast(I32).rearrange("q (a n) -> q a n", a=5)
+        nc.sync.dma_start(staged[:, 0:2, :], wt_scales.rearrange("a q n -> q a n").bitcast(I32))
+        nc.sync.dma_start(staged[:, 2:3, :], zv_scales.rearrange("a q n -> q a n").bitcast(I32))
+        nc.sync.dma_start(staged[:, 3:5, :], zt_scales.rearrange("a q n -> q a n").bitcast(I32))
+        with nc.allow_non_contiguous_dma(reason="one bias value for each partition"):
+            nc.sync.dma_start(b_sb[:], b.rearrange("(m p) -> p m", p=P))
+        nc.sync.dma_start(tab2_w[:], tab2_words[0].rearrange("p t i -> p (t i)").bitcast(I32))
+        nc.sync.dma_start(wt_w[:], wt_words.rearrange("a p n i -> p a (n i)").bitcast(I32))
+        nc.sync.dma_start(zv_w[:].bitcast(I32), zv_words[0].bitcast(I32))
+        nc.sync.dma_start(zt_w[:].bitcast(I32), zt_words.rearrange("a p c -> p a c").bitcast(I32))
+
+        for h in range(2):
+            nc.scalar.copy(out=wv_bf[:, h * (N // 2) : (h + 1) * (N // 2), :], in_=wv_raw[h][:].rearrange("p i n -> p n i"))
+        nc.scalar.mul(half_b[:], b_sb[:], 0.5)
+
+        nc.vector.tensor_copy(v2_s0[:], tab2_s[:].indirect(list2[:]))
+        nc.vector.tensor_copy(v_s[:], tab_s[:].indirect(list1[:]))
+        nc.scalar.dma_start(v2_s1[0:100, :].bitcast(I32), v2_s0[4:104, :].bitcast(I32))
+        for q in range(1, QUADS):
+            nc.scalar.dma_start(w_scales[32 * q : 32 * q + 4, :].bitcast(I32), w_scales[4 * q : 4 * q + 4, :].bitcast(I32))
+        nc.vector.quantize_mx(out=wv_codes[:].bitcast(FP8X4), scales=wv_scales[:], in_=wv_bf[:].rearrange("p n i -> p (n i)"))
+
+        cols = CHUNK // 16
+        v_w0 = keep.tile([P, CHUNK], U32, name="v_w0", align_bytes=64)
+        nc.vector.tensor_copy(v_w0[:], tab_w[:].bitcast(U32).indirect(list1[:, 0:cols]))
+        pair0 = keep.tile([P, CHUNK], U32, name="pair0", tag="shared", align_bytes=64)
+        pair1 = keep.tile([P, CHUNK], U32, name="pair1", align_bytes=64)
+        v2_w = [keep.tile([P, 2, CHUNK], U16, name="v2_w%d" % c, align_bytes=64) for c in range(2)]
+        nc.vector.tensor_copy(pair0[:], tab2_w[:].bitcast(U32).indirect(list2[:, 0:cols]))
+        nc.vector.tensor_copy(v2_w[0][:], pair0[:].bitcast(U16).rearrange("p (j d) -> p d j", d=2))
+        nc.vector.tensor_copy(pair1[:], tab2_w[:].bitcast(U32).indirect(list2[:, cols : 2 * cols]))
+        v_w1 = keep.tile([P, CHUNK], U32, name="v_w1", tag="shared", align_bytes=64)
+        nc.vector.tensor_copy(v_w1[:], tab_w[:].bitcast(U32).indirect(list1[:, cols : 2 * cols]))
+        nc.vector.tensor_copy(v2_w[1][:], pair1[:].bitcast(U16).rearrange("p (j d) -> p d j", d=2))
+        v_w = [v_w0, v_w1]
+        v2_s = [v2_s0, v2_s1]
+
+        for c in range(J // CHUNK):
+            js = slice(c * CHUNK, (c + 1) * CHUNK)
+            for m in range(N // P):
+                ns = slice(m * P, (m + 1) * P)
+
+                def w_scale(plane):
+                    return w_scales[:, plane * N + m * P : plane * N + (m + 1) * P]
+
+                fp4_cols = slice(2 * m * P, 2 * (m + 1) * P)
+                hv = psum.tile([P, CHUNK], F32, name="hv", bufs=2)
+                ht = psum.tile([P, CHUNK], F32, name="ht", bufs=3)
+                z = psum.tile([P, CHUNK], F32, name="z", bufs=3)
+                nc.tensor.matmul_mx(out=hv[:], lhsT=wv_codes[:, ns].bitcast(FP8X4), lhsT_scale=wv_scales[:, ns],
+                                    rhs=v_w[c][:].bitcast(FP8X4), rhs_scale=v_s[:, js], start=True, stop=True)
+                for a in range(2):
+                    nc.tensor.matmul_mx(out=ht[:], lhsT=wt_w[:, a, ns].bitcast(FP8X4), lhsT_scale=w_scale(a),
+                                        rhs=v2_w[c][:, a, :].bitcast(FP4X4), rhs_scale=v2_s[a][:, js],
+                                        start=(a == 0), stop=(a == 1))
+                nc.tensor.matmul_mx(out=z[:], lhsT=zv_w[:, fp4_cols].bitcast(FP4X4), lhsT_scale=w_scale(2),
+                                    rhs=v_w[c][:].bitcast(FP8X4), rhs_scale=v_s[:, js], start=True, stop=False)
+                for a in range(2):
+                    nc.tensor.matmul_mx(out=z[:], lhsT=zt_w[:, a, fp4_cols].bitcast(FP4X4), lhsT_scale=w_scale(3 + a),
+                                        rhs=v2_w[c][:, a, :].bitcast(FP4X4), rhs_scale=v2_s[a][:, js],
+                                        start=False, stop=(a == 1))
+
+                av = ring.tile([P, CHUNK], F32, name="av", bufs=4)
+                at = ring.tile([P, CHUNK], F32, name="at", bufs=4)
+                th = ring.tile([P, CHUNK], F32, name="th", bufs=4)
+                nc.scalar.activation(out=av[:], in_=hv[:], func=ACT.Silu)
+                nc.scalar.activation(out=at[:], in_=ht[:], func=ACT.Silu)
+                nc.scalar.activation(out=th[:], in_=z[:], func=ACT.Tanh, bias=half_b[:, m : m + 1], scale=0.5)
+
+                diff = ring.tile([P, CHUNK], F32, name="diff")
+                gated = ring.tile([P, CHUNK], F32, name="gated")
+                res = ring.tile([P, CHUNK], F32, name="res", bufs=4)
+                nc.vector.tensor_tensor(out=diff[:], in0=av[:], in1=at[:], op=ALU.subtract)
+                nc.vector.scalar_tensor_tensor(out=gated[:], in0=th[:], scalar=1.0, in1=diff[:], op0=ALU.add, op1=ALU.mult)
+                nc.vector.scalar_tensor_tensor(out=res[:], in0=gated[:], scalar=0.5, in1=at[:], op0=ALU.mult, op1=ALU.add)
+                nc.sync.dma_start(out[ns, js], res[:])

@@ -36,114 +36,120 @@ def tile_list_gmu_silu_none_kernel(
         list2 = keep.tile([P, J // 16], U16, name="list2")
         tab_w = keep.tile([P, T], I32, name="tab_w", align_bytes=64)
         tab2_w = keep.tile([P, T], I32, name="tab2_w", align_bytes=64)
-        tab_s = keep.tile([P, T], U8, name="tab_s", align_bytes=64)
+        tab_s = keep.tile([P, T], U8, name="tab_s", tag="tab_s", align_bytes=64)
         tab2_s = keep.tile([P, T], U8, name="tab2_s", align_bytes=64)
         w_scales = keep.tile([P, 5 * N], U8, name="w_scales", align_bytes=64)
         wt_w = keep.tile([P, 2, N], I32, name="wt_w", align_bytes=64)
         zv_w = keep.tile([P, 2 * N], U8, name="zv_w", align_bytes=64)
         zt_w = keep.tile([P, 2, 2 * N], U8, name="zt_w", align_bytes=64)
-        wv_raw = [keep.tile([P, PACK, N // 2], F32, name="wv_raw%d" % h, align_bytes=64) for h in range(2)]
+        wv_raw = keep.tile([P, PACK, N], F32, name="wv_raw", align_bytes=64)
         wv_bf = keep.tile([P, N, PACK], BF16, name="wv_bf", align_bytes=64)
-        wv_codes = keep.tile([P, N], U32, name="wv_codes", align_bytes=64)
         wv_scales = keep.tile([P, N], U8, name="wv_scales", align_bytes=64)
         b_sb = keep.tile([P, N // P], F32, name="b_sb")
         half_b = keep.tile([P, N // P], F32, name="half_b")
         v_s = keep.tile([P, J], U8, name="v_s", align_bytes=64)
         v2_s0 = keep.tile([P, J], U8, name="v2_s0", align_bytes=64)
-        v2_s1 = keep.tile([P, J], U8, name="v2_s1", align_bytes=64)
         warm_in = keep.tile([P, 1], F32, name="warm_in")
         warm_out = keep.tile([P, 1], F32, name="warm_out")
 
-        nc.vector.memset(tab2_s[:].bitcast(I32), 0)
+        nc.vector.memset(tab2_s[:, 0 : T // 2].bitcast(I32), 0)
+        nc.gpsimd.memset(tab2_s[:, T // 2 : T].bitcast(I32), 0)
+        nc.vector.memset(w_scales[:].bitcast(I32), 0)
         nc.vector.memset(tab_s[:].bitcast(I32), 0)
         nc.vector.memset(warm_in[:], 0.0)
-        nc.vector.memset(w_scales[:].bitcast(I32), 0)
-        nc.vector.memset(v2_s1[:].bitcast(I32), 0)
         nc.scalar.activation(out=warm_out[:], in_=warm_in[:], func=ACT.Silu)
 
-        wv_rows = wv.rearrange("(p i) n -> p i n", i=PACK)
+        staged = w_scales[0:16, :].bitcast(I32).rearrange("q (a n) -> q a n", a=5)
+        nc.gpsimd.dma_start(staged[:, 0:2, :], wt_scales.rearrange("a q n -> q a n").bitcast(I32))
+        nc.gpsimd.dma_start(staged[:, 2:3, :], zv_scales.rearrange("a q n -> q a n").bitcast(I32))
+        nc.gpsimd.dma_start(staged[:, 3:5, :], zt_scales.rearrange("a q n -> q a n").bitcast(I32))
+        with nc.allow_non_contiguous_dma(reason="one bias value for each partition"):
+            nc.gpsimd.dma_start(b_sb[:], b.rearrange("(m p) -> p m", p=P))
         nc.sync.dma_start(list2[:], offs2)
+        tab2_rows = tab2_scales.rearrange("a (q r) t -> r q a t", r=4).bitcast(I32)
+        for r in range(4):
+            nc.sync.dma_start(tab2_s[r:P:16, :].bitcast(I32), tab2_rows[r])
+        nc.sync.dma_start(wv_raw[:], wv.rearrange("(p i) n -> p i n", i=PACK))
         nc.sync.dma_start(list1[:], offs)
         for q in range(QUADS):
-            nc.sync.dma_start(tab2_s[32 * q : 32 * q + 8, :].bitcast(I32), tab2_scales[:, 4 * q : 4 * q + 4, :].bitcast(I32))
-        for h in range(2):
-            nc.sync.dma_start(wv_raw[h][:], wv_rows[:, :, h * (N // 2) : (h + 1) * (N // 2)])
-        for q in range(QUADS):
-            nc.gpsimd.dma_start(tab_s[32 * q : 32 * q + 4, :].bitcast(I32), tab_scales[0, 4 * q : 4 * q + 4, :].bitcast(I32))
+            nc.sync.dma_start(tab_s[32 * q : 32 * q + 4, :].bitcast(I32), tab_scales[0, 4 * q : 4 * q + 4, :].bitcast(I32))
         nc.sync.dma_start(tab_w[:], tab_words[0].rearrange("p t i -> p (t i)").bitcast(I32))
-        staged = w_scales[0:16, :].bitcast(I32).rearrange("q (a n) -> q a n", a=5)
-        nc.sync.dma_start(staged[:, 0:2, :], wt_scales.rearrange("a q n -> q a n").bitcast(I32))
-        nc.sync.dma_start(staged[:, 2:3, :], zv_scales.rearrange("a q n -> q a n").bitcast(I32))
-        nc.sync.dma_start(staged[:, 3:5, :], zt_scales.rearrange("a q n -> q a n").bitcast(I32))
-        with nc.allow_non_contiguous_dma(reason="one bias value for each partition"):
-            nc.sync.dma_start(b_sb[:], b.rearrange("(m p) -> p m", p=P))
         nc.sync.dma_start(tab2_w[:], tab2_words[0].rearrange("p t i -> p (t i)").bitcast(I32))
         nc.sync.dma_start(wt_w[:], wt_words.rearrange("a p n i -> p a (n i)").bitcast(I32))
-        nc.sync.dma_start(zv_w[:].bitcast(I32), zv_words[0].bitcast(I32))
         nc.sync.dma_start(zt_w[:].bitcast(I32), zt_words.rearrange("a p c -> p a c").bitcast(I32))
+        nc.sync.dma_start(zv_w[:].bitcast(I32), zv_words[0].bitcast(I32))
+        for q in range(1, QUADS):
+            nc.sync.dma_start(w_scales[32 * q : 32 * q + 4, :].bitcast(I32), w_scales[4 * q : 4 * q + 4, :].bitcast(I32))
 
-        for h in range(2):
-            nc.scalar.copy(out=wv_bf[:, h * (N // 2) : (h + 1) * (N // 2), :], in_=wv_raw[h][:].rearrange("p i n -> p n i"))
+        nc.scalar.copy(out=wv_bf[:], in_=wv_raw[:].rearrange("p i n -> p n i"))
         nc.scalar.mul(half_b[:], b_sb[:], 0.5)
 
         nc.vector.tensor_copy(v2_s0[:], tab2_s[:].indirect(list2[:]))
         nc.vector.tensor_copy(v_s[:], tab_s[:].indirect(list1[:]))
-        nc.scalar.dma_start(v2_s1[0:100, :].bitcast(I32), v2_s0[4:104, :].bitcast(I32))
-        for q in range(1, QUADS):
-            nc.scalar.dma_start(w_scales[32 * q : 32 * q + 4, :].bitcast(I32), w_scales[4 * q : 4 * q + 4, :].bitcast(I32))
-        nc.vector.quantize_mx(out=wv_codes[:].bitcast(FP8X4), scales=wv_scales[:], in_=wv_bf[:].rearrange("p n i -> p (n i)"))
+
+        late = keep.tile([P, N + J // 4], I32, name="late", tag="tab_s", align_bytes=64)
+        wv_codes = late[:, 0:N]
+        nc.vector.memset(late[:, N:], 0)
+        nc.scalar.dma_start(late[0:112, N:], v2_s0[16:P, :].bitcast(I32))
+        v2_s1 = late[:, N:].bitcast(U8)
+        nc.vector.quantize_mx(out=wv_codes.bitcast(FP8X4), scales=wv_scales[:], in_=wv_bf[:].rearrange("p n i -> p (n i)"))
 
         cols = CHUNK // 16
-        v_w0 = keep.tile([P, CHUNK], U32, name="v_w0", align_bytes=64)
-        nc.vector.tensor_copy(v_w0[:], tab_w[:].bitcast(U32).indirect(list1[:, 0:cols]))
-        pair0 = keep.tile([P, CHUNK], U32, name="pair0", tag="shared", align_bytes=64)
-        pair1 = keep.tile([P, CHUNK], U32, name="pair1", align_bytes=64)
         v2_w = [keep.tile([P, 2, CHUNK], U16, name="v2_w%d" % c, align_bytes=64) for c in range(2)]
+        v_w0 = keep.tile([P, CHUNK], U32, name="v_w0", align_bytes=64)
+        pair0 = keep.tile([P, CHUNK], U32, name="pair0", tag="picked", align_bytes=64)
+        nc.vector.tensor_copy(v_w0[:], tab_w[:].bitcast(U32).indirect(list1[:, 0:cols]))
         nc.vector.tensor_copy(pair0[:], tab2_w[:].bitcast(U32).indirect(list2[:, 0:cols]))
         nc.vector.tensor_copy(v2_w[0][:], pair0[:].bitcast(U16).rearrange("p (j d) -> p d j", d=2))
-        nc.vector.tensor_copy(pair1[:], tab2_w[:].bitcast(U32).indirect(list2[:, cols : 2 * cols]))
-        v_w1 = keep.tile([P, CHUNK], U32, name="v_w1", tag="shared", align_bytes=64)
-        nc.vector.tensor_copy(v_w1[:], tab_w[:].bitcast(U32).indirect(list1[:, cols : 2 * cols]))
-        nc.vector.tensor_copy(v2_w[1][:], pair1[:].bitcast(U16).rearrange("p (j d) -> p d j", d=2))
-        v_w = [v_w0, v_w1]
+        second = keep.tile([P, 2 * CHUNK], U32, name="second", tag="picked", align_bytes=64)
+        pair1 = second[:, 0:CHUNK]
+        nc.vector.tensor_copy(pair1, tab2_w[:].bitcast(U32).indirect(list2[:, cols : 2 * cols]))
+        nc.vector.tensor_copy(second[:, CHUNK:], tab_w[:].bitcast(U32).indirect(list1[:, cols : 2 * cols]))
+        nc.vector.tensor_copy(v2_w[1][:], pair1.bitcast(U16).rearrange("p (j d) -> p d j", d=2))
+        v_w = [v_w0[:], second[:, CHUNK:]]
         v2_s = [v2_s0, v2_s1]
+
+        def w_scale(plane, m):
+            return w_scales[:, plane * N + m * P : plane * N + (m + 1) * P]
 
         for c in range(J // CHUNK):
             js = slice(c * CHUNK, (c + 1) * CHUNK)
-            for m in range(N // P):
-                ns = slice(m * P, (m + 1) * P)
+            for m0 in range(0, N // P, 2):
+                ms = (m0, m0 + 1)
+                av = ring.tile([P, 2, CHUNK], F32, name="av", bufs=2)
+                at = ring.tile([P, 2, CHUNK], F32, name="at", bufs=2)
+                th = ring.tile([P, 2, CHUNK], F32, name="th", bufs=2)
+                for i, m in enumerate(ms):
+                    ns = slice(m * P, (m + 1) * P)
+                    hv = psum.tile([P, CHUNK], F32, name="hv", bufs=3)
+                    nc.tensor.matmul_mx(out=hv[:], lhsT=wv_codes[:, ns].bitcast(FP8X4), lhsT_scale=wv_scales[:, ns],
+                                        rhs=v_w[c].bitcast(FP8X4), rhs_scale=v_s[:, js], start=True, stop=True)
+                    nc.scalar.activation(out=av[:, i, :], in_=hv[:], func=ACT.Silu)
+                for i, m in enumerate(ms):
+                    ns = slice(m * P, (m + 1) * P)
+                    ht = psum.tile([P, CHUNK], F32, name="ht", bufs=2)
+                    for a in (1, 0):
+                        nc.tensor.matmul_mx(out=ht[:], lhsT=wt_w[:, a, ns].bitcast(FP8X4), lhsT_scale=w_scale(a, m),
+                                            rhs=v2_w[c][:, a, :].bitcast(FP4X4), rhs_scale=v2_s[a][:, js],
+                                            start=(a == 1), stop=(a == 0))
+                    nc.scalar.activation(out=at[:, i, :], in_=ht[:], func=ACT.Silu)
+                for i, m in enumerate(ms):
+                    fp4_cols = slice(2 * m * P, 2 * (m + 1) * P)
+                    z = psum.tile([P, CHUNK], F32, name="z", bufs=3)
+                    for a in (1, 0):
+                        nc.tensor.matmul_mx(out=z[:], lhsT=zt_w[:, a, fp4_cols].bitcast(FP4X4), lhsT_scale=w_scale(3 + a, m),
+                                            rhs=v2_w[c][:, a, :].bitcast(FP4X4), rhs_scale=v2_s[a][:, js],
+                                            start=(a == 1), stop=False)
+                    nc.tensor.matmul_mx(out=z[:], lhsT=zv_w[:, fp4_cols].bitcast(FP4X4), lhsT_scale=w_scale(2, m),
+                                        rhs=v_w[c].bitcast(FP8X4), rhs_scale=v_s[:, js], start=False, stop=True)
+                    nc.scalar.activation(out=th[:, i, :], in_=z[:], func=ACT.Tanh, bias=half_b[:, m : m + 1], scale=0.5)
 
-                def w_scale(plane):
-                    return w_scales[:, plane * N + m * P : plane * N + (m + 1) * P]
-
-                fp4_cols = slice(2 * m * P, 2 * (m + 1) * P)
-                hv = psum.tile([P, CHUNK], F32, name="hv", bufs=2)
-                ht = psum.tile([P, CHUNK], F32, name="ht", bufs=3)
-                z = psum.tile([P, CHUNK], F32, name="z", bufs=3)
-                nc.tensor.matmul_mx(out=hv[:], lhsT=wv_codes[:, ns].bitcast(FP8X4), lhsT_scale=wv_scales[:, ns],
-                                    rhs=v_w[c][:].bitcast(FP8X4), rhs_scale=v_s[:, js], start=True, stop=True)
-                for a in range(2):
-                    nc.tensor.matmul_mx(out=ht[:], lhsT=wt_w[:, a, ns].bitcast(FP8X4), lhsT_scale=w_scale(a),
-                                        rhs=v2_w[c][:, a, :].bitcast(FP4X4), rhs_scale=v2_s[a][:, js],
-                                        start=(a == 0), stop=(a == 1))
-                nc.tensor.matmul_mx(out=z[:], lhsT=zv_w[:, fp4_cols].bitcast(FP4X4), lhsT_scale=w_scale(2),
-                                    rhs=v_w[c][:].bitcast(FP8X4), rhs_scale=v_s[:, js], start=True, stop=False)
-                for a in range(2):
-                    nc.tensor.matmul_mx(out=z[:], lhsT=zt_w[:, a, fp4_cols].bitcast(FP4X4), lhsT_scale=w_scale(3 + a),
-                                        rhs=v2_w[c][:, a, :].bitcast(FP4X4), rhs_scale=v2_s[a][:, js],
-                                        start=False, stop=(a == 1))
-
-                av = ring.tile([P, CHUNK], F32, name="av", bufs=4)
-                at = ring.tile([P, CHUNK], F32, name="at", bufs=4)
-                th = ring.tile([P, CHUNK], F32, name="th", bufs=4)
-                nc.scalar.activation(out=av[:], in_=hv[:], func=ACT.Silu)
-                nc.scalar.activation(out=at[:], in_=ht[:], func=ACT.Silu)
-                nc.scalar.activation(out=th[:], in_=z[:], func=ACT.Tanh, bias=half_b[:, m : m + 1], scale=0.5)
-
-                diff = ring.tile([P, CHUNK], F32, name="diff")
-                gated = ring.tile([P, CHUNK], F32, name="gated")
-                res = ring.tile([P, CHUNK], F32, name="res", bufs=4)
+                diff = ring.tile([P, 2, CHUNK], F32, name="diff", bufs=2)
+                gated = ring.tile([P, 2, CHUNK], F32, name="gated", bufs=2)
                 nc.vector.tensor_tensor(out=diff[:], in0=av[:], in1=at[:], op=ALU.subtract)
-                nc.vector.scalar_tensor_tensor(out=gated[:], in0=th[:], scalar=1.0, in1=diff[:], op0=ALU.add, op1=ALU.mult)
-                nc.vector.scalar_tensor_tensor(out=res[:], in0=gated[:], scalar=0.5, in1=at[:], op0=ALU.mult, op1=ALU.add)
-                nc.sync.dma_start(out[ns, js], res[:])
+                for i in range(2):
+                    nc.vector.scalar_tensor_tensor(out=gated[:, i, :], in0=th[:, i, :], scalar=1.0, in1=diff[:, i, :], op0=ALU.add, op1=ALU.mult)
+                for i, m in enumerate(ms):
+                    res = ring.tile([P, CHUNK], F32, name="res", bufs=4)
+                    nc.vector.scalar_tensor_tensor(out=res[:], in0=gated[:, i, :], scalar=0.5, in1=at[:, i, :], op0=ALU.mult, op1=ALU.add)
+                    nc.sync.dma_start(out[m * P : (m + 1) * P, js], res[:])

@@ -49,23 +49,21 @@ def tile_list_gmu_silu_none_kernel(
         half_b = keep.tile([P, N // P], F32, name="half_b")
         v_s = keep.tile([P, J], U8, name="v_s", align_bytes=64)
         v2_s0 = keep.tile([P, J], U8, name="v2_s0", align_bytes=64)
+        v2_s1 = keep.tile([P, J], U8, name="v2_s1", align_bytes=64)
         warm_in = keep.tile([P, 1], F32, name="warm_in")
         warm_out = keep.tile([P, 1], F32, name="warm_out")
 
         nc.vector.memset(tab2_s[:, 0 : T // 2].bitcast(I32), 0)
         nc.gpsimd.memset(tab2_s[:, T // 2 : T].bitcast(I32), 0)
-        nc.vector.memset(w_scales[:].bitcast(I32), 0)
-        nc.vector.memset(tab_s[:].bitcast(I32), 0)
         nc.vector.memset(warm_in[:], 0.0)
+        nc.vector.memset(tab_s[:].bitcast(I32), 0)
+        nc.vector.memset(w_scales[:].bitcast(I32), 0)
+        nc.vector.memset(v2_s1[:].bitcast(I32), 0)
         nc.scalar.activation(out=warm_out[:], in_=warm_in[:], func=ACT.Silu)
 
-        staged = w_scales[0:16, :].bitcast(I32).rearrange("q (a n) -> q a n", a=5)
-        nc.gpsimd.dma_start(staged[:, 0:2, :], wt_scales.rearrange("a q n -> q a n").bitcast(I32))
-        nc.gpsimd.dma_start(staged[:, 2:3, :], zv_scales.rearrange("a q n -> q a n").bitcast(I32))
-        nc.gpsimd.dma_start(staged[:, 3:5, :], zt_scales.rearrange("a q n -> q a n").bitcast(I32))
-        with nc.allow_non_contiguous_dma(reason="one bias value for each partition"):
-            nc.gpsimd.dma_start(b_sb[:], b.rearrange("(m p) -> p m", p=P))
         nc.sync.dma_start(list2[:], offs2)
+        with nc.allow_non_contiguous_dma(reason="one bias value for each partition"):
+            nc.sync.dma_start(b_sb[:], b.rearrange("(m p) -> p m", p=P))
         tab2_rows = tab2_scales.rearrange("a (q r) t -> r q a t", r=4).bitcast(I32)
         for r in range(4):
             nc.sync.dma_start(tab2_s[r:P:16, :].bitcast(I32), tab2_rows[r])
@@ -74,25 +72,26 @@ def tile_list_gmu_silu_none_kernel(
         for q in range(QUADS):
             nc.sync.dma_start(tab_s[32 * q : 32 * q + 4, :].bitcast(I32), tab_scales[0, 4 * q : 4 * q + 4, :].bitcast(I32))
         nc.sync.dma_start(tab_w[:], tab_words[0].rearrange("p t i -> p (t i)").bitcast(I32))
+        staged = w_scales[0:16, :].bitcast(I32).rearrange("q (a n) -> q a n", a=5)
+        nc.sync.dma_start(staged[:, 0:2, :], wt_scales.rearrange("a q n -> q a n").bitcast(I32))
+        nc.sync.dma_start(staged[:, 2:3, :], zv_scales.rearrange("a q n -> q a n").bitcast(I32))
+        nc.sync.dma_start(staged[:, 3:5, :], zt_scales.rearrange("a q n -> q a n").bitcast(I32))
         nc.sync.dma_start(tab2_w[:], tab2_words[0].rearrange("p t i -> p (t i)").bitcast(I32))
-        nc.sync.dma_start(wt_w[:], wt_words.rearrange("a p n i -> p a (n i)").bitcast(I32))
-        nc.sync.dma_start(zt_w[:].bitcast(I32), zt_words.rearrange("a p c -> p a c").bitcast(I32))
-        nc.sync.dma_start(zv_w[:].bitcast(I32), zv_words[0].bitcast(I32))
-        for q in range(1, QUADS):
-            nc.sync.dma_start(w_scales[32 * q : 32 * q + 4, :].bitcast(I32), w_scales[4 * q : 4 * q + 4, :].bitcast(I32))
 
-        nc.scalar.copy(out=wv_bf[:], in_=wv_raw[:].rearrange("p i n -> p n i"))
         nc.scalar.mul(half_b[:], b_sb[:], 0.5)
-
+        nc.scalar.copy(out=wv_bf[:], in_=wv_raw[:].rearrange("p i n -> p n i"))
         nc.vector.tensor_copy(v2_s0[:], tab2_s[:].indirect(list2[:]))
         nc.vector.tensor_copy(v_s[:], tab_s[:].indirect(list1[:]))
 
-        late = keep.tile([P, N + J // 4], I32, name="late", tag="tab_s", align_bytes=64)
-        wv_codes = late[:, 0:N]
-        nc.vector.memset(late[:, N:], 0)
-        nc.scalar.dma_start(late[0:112, N:], v2_s0[16:P, :].bitcast(I32))
-        v2_s1 = late[:, N:].bitcast(U8)
-        nc.vector.quantize_mx(out=wv_codes.bitcast(FP8X4), scales=wv_scales[:], in_=wv_bf[:].rearrange("p n i -> p (n i)"))
+        nc.sync.dma_start(v2_s1[0:112, :].bitcast(I32), v2_s0[16:P, :].bitcast(I32))
+        for q in range(1, QUADS):
+            nc.sync.dma_start(w_scales[32 * q : 32 * q + 4, :].bitcast(I32), w_scales[4 * q : 4 * q + 4, :].bitcast(I32))
+        nc.sync.dma_start(wt_w[:], wt_words.rearrange("a p n i -> p a (n i)").bitcast(I32))
+        nc.sync.dma_start(zt_w[:].bitcast(I32), zt_words.rearrange("a p c -> p a c").bitcast(I32))
+        nc.sync.dma_start(zv_w[:].bitcast(I32), zv_words[0].bitcast(I32))
+
+        wv_codes = keep.tile([P, N], U32, name="wv_codes", tag="tab_s", align_bytes=64)
+        nc.vector.quantize_mx(out=wv_codes[:].bitcast(FP8X4), scales=wv_scales[:], in_=wv_bf[:].rearrange("p n i -> p (n i)"))
 
         cols = CHUNK // 16
         v2_w = [keep.tile([P, 2, CHUNK], U16, name="v2_w%d" % c, align_bytes=64) for c in range(2)]
@@ -121,13 +120,13 @@ def tile_list_gmu_silu_none_kernel(
                 th = ring.tile([P, 2, CHUNK], F32, name="th", bufs=2)
                 for i, m in enumerate(ms):
                     ns = slice(m * P, (m + 1) * P)
-                    hv = psum.tile([P, CHUNK], F32, name="hv", bufs=3)
+                    hv = psum.tile([P, CHUNK], F32, name="hv", tag="acc", bufs=6)
                     nc.tensor.matmul_mx(out=hv[:], lhsT=wv_codes[:, ns].bitcast(FP8X4), lhsT_scale=wv_scales[:, ns],
                                         rhs=v_w[c].bitcast(FP8X4), rhs_scale=v_s[:, js], start=True, stop=True)
                     nc.scalar.activation(out=av[:, i, :], in_=hv[:], func=ACT.Silu)
                 for i, m in enumerate(ms):
                     ns = slice(m * P, (m + 1) * P)
-                    ht = psum.tile([P, CHUNK], F32, name="ht", bufs=2)
+                    ht = psum.tile([P, CHUNK], F32, name="ht", tag="acc", bufs=6)
                     for a in (1, 0):
                         nc.tensor.matmul_mx(out=ht[:], lhsT=wt_w[:, a, ns].bitcast(FP8X4), lhsT_scale=w_scale(a, m),
                                             rhs=v2_w[c][:, a, :].bitcast(FP4X4), rhs_scale=v2_s[a][:, js],
@@ -135,7 +134,7 @@ def tile_list_gmu_silu_none_kernel(
                     nc.scalar.activation(out=at[:, i, :], in_=ht[:], func=ACT.Silu)
                 for i, m in enumerate(ms):
                     fp4_cols = slice(2 * m * P, 2 * (m + 1) * P)
-                    z = psum.tile([P, CHUNK], F32, name="z", bufs=3)
+                    z = psum.tile([P, CHUNK], F32, name="z", tag="acc", bufs=6)
                     for a in (1, 0):
                         nc.tensor.matmul_mx(out=z[:], lhsT=zt_w[:, a, fp4_cols].bitcast(FP4X4), lhsT_scale=w_scale(3 + a, m),
                                             rhs=v2_w[c][:, a, :].bitcast(FP4X4), rhs_scale=v2_s[a][:, js],

@@ -20,6 +20,8 @@ P = 128
 PACK = 4
 CHUNK = 512
 QUADS = 4
+MS = N // P
+TILES = MS * (J // CHUNK)
 
 
 def tile_list_gmu_silu_none_kernel(
@@ -36,7 +38,7 @@ def tile_list_gmu_silu_none_kernel(
         list2 = keep.tile([P, J // 16], U16, name="list2")
         tab_w = keep.tile([P, T], I32, name="tab_w", align_bytes=64)
         tab2_w = keep.tile([P, T], I32, name="tab2_w", align_bytes=64)
-        tab_s = keep.tile([P, T], U8, name="tab_s", tag="tab_s", align_bytes=64)
+        tab_s = keep.tile([P, T], U8, name="tab_s", align_bytes=64)
         tab2_s = keep.tile([P, T], U8, name="tab2_s", align_bytes=64)
         w_scales = keep.tile([P, 5 * N], U8, name="w_scales", align_bytes=64)
         wt_w = keep.tile([P, 2, N], I32, name="wt_w", align_bytes=64)
@@ -45,110 +47,139 @@ def tile_list_gmu_silu_none_kernel(
         wv_raw = keep.tile([P, PACK, N], F32, name="wv_raw", align_bytes=64)
         wv_bf = keep.tile([P, N, PACK], BF16, name="wv_bf", align_bytes=64)
         wv_scales = keep.tile([P, N], U8, name="wv_scales", align_bytes=64)
-        b_sb = keep.tile([P, N // P], F32, name="b_sb")
-        half_b = keep.tile([P, N // P], F32, name="half_b")
+        b_sb = keep.tile([P, MS], F32, name="b_sb")
+        half_b = keep.tile([P, MS], F32, name="half_b")
         v_s = keep.tile([P, J], U8, name="v_s", align_bytes=64)
         v2_s0 = keep.tile([P, J], U8, name="v2_s0", align_bytes=64)
         v2_s1 = keep.tile([P, J], U8, name="v2_s1", align_bytes=64)
+        v_w = [keep.tile([P, CHUNK], U32, name="v_w%d" % c, align_bytes=64) for c in range(2)]
+        v2_w = [keep.tile([P, 2, CHUNK], U16, name="v2_w%d" % c, align_bytes=64) for c in range(2)]
+        av = [keep.tile([P, CHUNK], F32, name="av%d" % i) for i in range(TILES)]
+
         warm_in = keep.tile([P, 1], F32, name="warm_in")
         warm_out = keep.tile([P, 1], F32, name="warm_out")
-
+        pair = [keep.tile([P, CHUNK], U32, name="pair%d" % c, align_bytes=64) for c in range(2)]
+        wv_codes = keep.tile([P, N], U32, name="wv_codes", align_bytes=64)
         nc.vector.memset(tab2_s[:, 0 : T // 2].bitcast(I32), 0)
         nc.gpsimd.memset(tab2_s[:, T // 2 : T].bitcast(I32), 0)
         nc.vector.memset(warm_in[:], 0.0)
+        nc.scalar.activation(out=warm_out[:], in_=warm_in[:], func=ACT.Silu)
         nc.vector.memset(tab_s[:].bitcast(I32), 0)
         nc.vector.memset(w_scales[:].bitcast(I32), 0)
         nc.vector.memset(v2_s1[:].bitcast(I32), 0)
-        nc.scalar.activation(out=warm_out[:], in_=warm_in[:], func=ACT.Silu)
 
+        cols = CHUNK // 16
+        planes = w_scales[:].bitcast(I32).rearrange("p (a n) -> p a n", a=5)
         nc.sync.dma_start(list2[:], offs2)
         with nc.allow_non_contiguous_dma(reason="one bias value for each partition"):
             nc.sync.dma_start(b_sb[:], b.rearrange("(m p) -> p m", p=P))
         tab2_rows = tab2_scales.rearrange("a (q r) t -> r q a t", r=4).bitcast(I32)
         for r in range(4):
             nc.sync.dma_start(tab2_s[r:P:16, :].bitcast(I32), tab2_rows[r])
-        nc.sync.dma_start(wv_raw[:], wv.rearrange("(p i) n -> p i n", i=PACK))
-        nc.sync.dma_start(list1[:], offs)
-        for q in range(QUADS):
-            nc.sync.dma_start(tab_s[32 * q : 32 * q + 4, :].bitcast(I32), tab_scales[0, 4 * q : 4 * q + 4, :].bitcast(I32))
-        nc.sync.dma_start(tab_w[:], tab_words[0].rearrange("p t i -> p (t i)").bitcast(I32))
-        staged = w_scales[0:16, :].bitcast(I32).rearrange("q (a n) -> q a n", a=5)
-        nc.sync.dma_start(staged[:, 0:2, :], wt_scales.rearrange("a q n -> q a n").bitcast(I32))
-        nc.sync.dma_start(staged[:, 2:3, :], zv_scales.rearrange("a q n -> q a n").bitcast(I32))
-        nc.sync.dma_start(staged[:, 3:5, :], zt_scales.rearrange("a q n -> q a n").bitcast(I32))
         nc.sync.dma_start(tab2_w[:], tab2_words[0].rearrange("p t i -> p (t i)").bitcast(I32))
-
-        nc.scalar.mul(half_b[:], b_sb[:], 0.5)
-        nc.scalar.copy(out=wv_bf[:], in_=wv_raw[:].rearrange("p i n -> p n i"))
-        nc.vector.tensor_copy(v2_s0[:], tab2_s[:].indirect(list2[:]))
-        nc.vector.tensor_copy(v_s[:], tab_s[:].indirect(list1[:]))
-
-        nc.sync.dma_start(v2_s1[0:112, :].bitcast(I32), v2_s0[16:P, :].bitcast(I32))
-        for q in range(1, QUADS):
-            nc.sync.dma_start(w_scales[32 * q : 32 * q + 4, :].bitcast(I32), w_scales[4 * q : 4 * q + 4, :].bitcast(I32))
         nc.sync.dma_start(wt_w[:], wt_words.rearrange("a p n i -> p a (n i)").bitcast(I32))
+        nc.sync.dma_start(list1[:], offs)
+        tab_rows = tab_scales[0].rearrange("(q r) t -> r q t", r=4).bitcast(I32)
+        for r in range(4):
+            nc.sync.dma_start(tab_s[r:P:32, :].bitcast(I32), tab_rows[r])
+        nc.sync.dma_start(wv_raw[:], wv.rearrange("(p i) n -> p i n", i=PACK))
+        nc.vector.tensor_copy(v2_s0[:], tab2_s[:].indirect(list2[:]))
+        nc.sync.dma_start(v2_s1[0:112, :].bitcast(I32), v2_s0[16:P, :].bitcast(I32))
+        wt_rows = wt_scales.rearrange("a (q r) n -> r q a n", r=4).bitcast(I32)
+        for r in range(4):
+            nc.sync.dma_start(planes[r:P:32, 0:2, :], wt_rows[r])
+        nc.sync.dma_start(tab_w[:], tab_words[0].rearrange("p t i -> p (t i)").bitcast(I32))
+        nc.sync.dma_start(planes[0:16, 2:3, :], zv_scales.rearrange("a q n -> q a n").bitcast(I32))
+        nc.sync.dma_start(planes[0:16, 3:5, :], zt_scales.rearrange("a q n -> q a n").bitcast(I32))
         nc.sync.dma_start(zt_w[:].bitcast(I32), zt_words.rearrange("a p c -> p a c").bitcast(I32))
         nc.sync.dma_start(zv_w[:].bitcast(I32), zv_words[0].bitcast(I32))
+        for q in range(1, QUADS):
+            nc.sync.dma_start(planes[32 * q : 32 * q + 4, 2:5, :], planes[4 * q : 4 * q + 4, 2:5, :])
 
-        wv_codes = keep.tile([P, N], U32, name="wv_codes", tag="tab_s", align_bytes=64)
+        nc.scalar.mul(half_b[:], b_sb[:], 0.5)
+        nc.scalar.copy(out=wv_bf[:].rearrange("p (c i) t -> p c t i", i=4),
+                       in_=wv_raw[:].rearrange("p t (c i) -> p c t i", i=4))
+        for c in range(2):
+            nc.vector.tensor_copy(pair[c][:], tab2_w[:].bitcast(U32).indirect(list2[:, c * cols : (c + 1) * cols]))
+        for c in range(2):
+            nc.vector.tensor_copy(v2_w[c][:], pair[c][:].bitcast(U16).rearrange("p (j d) -> p d j", d=2))
+        nc.vector.tensor_copy(v_s[:], tab_s[:].indirect(list1[:]))
         nc.vector.quantize_mx(out=wv_codes[:].bitcast(FP8X4), scales=wv_scales[:], in_=wv_bf[:].rearrange("p n i -> p (n i)"))
-
-        cols = CHUNK // 16
-        v2_w = [keep.tile([P, 2, CHUNK], U16, name="v2_w%d" % c, align_bytes=64) for c in range(2)]
-        v_w0 = keep.tile([P, CHUNK], U32, name="v_w0", align_bytes=64)
-        pair0 = keep.tile([P, CHUNK], U32, name="pair0", tag="picked", align_bytes=64)
-        nc.vector.tensor_copy(v_w0[:], tab_w[:].bitcast(U32).indirect(list1[:, 0:cols]))
-        nc.vector.tensor_copy(pair0[:], tab2_w[:].bitcast(U32).indirect(list2[:, 0:cols]))
-        nc.vector.tensor_copy(v2_w[0][:], pair0[:].bitcast(U16).rearrange("p (j d) -> p d j", d=2))
-        second = keep.tile([P, 2 * CHUNK], U32, name="second", tag="picked", align_bytes=64)
-        pair1 = second[:, 0:CHUNK]
-        nc.vector.tensor_copy(pair1, tab2_w[:].bitcast(U32).indirect(list2[:, cols : 2 * cols]))
-        nc.vector.tensor_copy(second[:, CHUNK:], tab_w[:].bitcast(U32).indirect(list1[:, cols : 2 * cols]))
-        nc.vector.tensor_copy(v2_w[1][:], pair1.bitcast(U16).rearrange("p (j d) -> p d j", d=2))
-        v_w = [v_w0[:], second[:, CHUNK:]]
+        for c in range(2):
+            nc.vector.tensor_copy(v_w[c][:], tab_w[:].bitcast(U32).indirect(list1[:, c * cols : (c + 1) * cols]))
         v2_s = [v2_s0, v2_s1]
 
         def w_scale(plane, m):
             return w_scales[:, plane * N + m * P : plane * N + (m + 1) * P]
 
-        for c in range(J // CHUNK):
-            js = slice(c * CHUNK, (c + 1) * CHUNK)
-            for m0 in range(0, N // P, 2):
-                ms = (m0, m0 + 1)
-                av = ring.tile([P, 2, CHUNK], F32, name="av", bufs=2)
-                at = ring.tile([P, 2, CHUNK], F32, name="at", bufs=2)
-                th = ring.tile([P, 2, CHUNK], F32, name="th", bufs=2)
-                for i, m in enumerate(ms):
-                    ns = slice(m * P, (m + 1) * P)
-                    hv = psum.tile([P, CHUNK], F32, name="hv", tag="acc", bufs=6)
-                    nc.tensor.matmul_mx(out=hv[:], lhsT=wv_codes[:, ns].bitcast(FP8X4), lhsT_scale=wv_scales[:, ns],
-                                        rhs=v_w[c].bitcast(FP8X4), rhs_scale=v_s[:, js], start=True, stop=True)
-                    nc.scalar.activation(out=av[:, i, :], in_=hv[:], func=ACT.Silu)
-                for i, m in enumerate(ms):
-                    ns = slice(m * P, (m + 1) * P)
-                    ht = psum.tile([P, CHUNK], F32, name="ht", tag="acc", bufs=6)
-                    for a in (1, 0):
-                        nc.tensor.matmul_mx(out=ht[:], lhsT=wt_w[:, a, ns].bitcast(FP8X4), lhsT_scale=w_scale(a, m),
-                                            rhs=v2_w[c][:, a, :].bitcast(FP4X4), rhs_scale=v2_s[a][:, js],
-                                            start=(a == 1), stop=(a == 0))
-                    nc.scalar.activation(out=at[:, i, :], in_=ht[:], func=ACT.Silu)
-                for i, m in enumerate(ms):
-                    fp4_cols = slice(2 * m * P, 2 * (m + 1) * P)
-                    z = psum.tile([P, CHUNK], F32, name="z", tag="acc", bufs=6)
-                    for a in (1, 0):
-                        nc.tensor.matmul_mx(out=z[:], lhsT=zt_w[:, a, fp4_cols].bitcast(FP4X4), lhsT_scale=w_scale(3 + a, m),
-                                            rhs=v2_w[c][:, a, :].bitcast(FP4X4), rhs_scale=v2_s[a][:, js],
-                                            start=(a == 1), stop=False)
-                    nc.tensor.matmul_mx(out=z[:], lhsT=zv_w[:, fp4_cols].bitcast(FP4X4), lhsT_scale=w_scale(2, m),
-                                        rhs=v_w[c].bitcast(FP8X4), rhs_scale=v_s[:, js], start=False, stop=True)
-                    nc.scalar.activation(out=th[:, i, :], in_=z[:], func=ACT.Tanh, bias=half_b[:, m : m + 1], scale=0.5)
+        at, th, diff, gated = {}, {}, {}, {}
 
-                diff = ring.tile([P, 2, CHUNK], F32, name="diff", bufs=2)
-                gated = ring.tile([P, 2, CHUNK], F32, name="gated", bufs=2)
-                nc.vector.tensor_tensor(out=diff[:], in0=av[:], in1=at[:], op=ALU.subtract)
-                for i in range(2):
-                    nc.vector.scalar_tensor_tensor(out=gated[:, i, :], in0=th[:, i, :], scalar=1.0, in1=diff[:, i, :], op0=ALU.add, op1=ALU.mult)
-                for i, m in enumerate(ms):
-                    res = ring.tile([P, CHUNK], F32, name="res", bufs=4)
-                    nc.vector.scalar_tensor_tensor(out=res[:], in0=gated[:, i, :], scalar=0.5, in1=at[:, i, :], op0=ALU.mult, op1=ALU.add)
-                    nc.sync.dma_start(out[m * P : (m + 1) * P, js], res[:])
+        def place(i):
+            c, m = divmod(i, MS)
+            return c, m, slice(c * CHUNK, (c + 1) * CHUNK), slice(m * P, (m + 1) * P)
+
+        def picture(i):
+            c, m, js, ns = place(i)
+            hv = psum.tile([P, CHUNK], F32, name="hv", tag="acc", bufs=8)
+            nc.tensor.matmul_mx(out=hv[:], lhsT=wv_codes[:, ns].bitcast(FP8X4), lhsT_scale=wv_scales[:, ns],
+                                rhs=v_w[c][:].bitcast(FP8X4), rhs_scale=v_s[:, js], start=True, stop=True)
+            nc.scalar.activation(out=av[i][:], in_=hv[:], func=ACT.Silu)
+
+        def text(i):
+            c, m, js, ns = place(i)
+            ht = psum.tile([P, CHUNK], F32, name="ht", tag="acc", bufs=8)
+            for a in range(2):
+                nc.tensor.matmul_mx(out=ht[:], lhsT=wt_w[:, a, ns].bitcast(FP8X4), lhsT_scale=w_scale(a, m),
+                                    rhs=v2_w[c][:, a, :].bitcast(FP4X4), rhs_scale=v2_s[a][:, js],
+                                    start=(a == 0), stop=(a == 1))
+            at[i] = ring.tile([P, CHUNK], F32, name="at", bufs=8)
+            nc.scalar.activation(out=at[i][:], in_=ht[:], func=ACT.Silu)
+
+        def gate(i):
+            c, m, js, ns = place(i)
+            fp4_cols = slice(2 * m * P, 2 * (m + 1) * P)
+            z = psum.tile([P, CHUNK], F32, name="z", tag="acc", bufs=8)
+            nc.tensor.matmul_mx(out=z[:], lhsT=zv_w[:, fp4_cols].bitcast(FP4X4), lhsT_scale=w_scale(2, m),
+                                rhs=v_w[c][:].bitcast(FP8X4), rhs_scale=v_s[:, js], start=True, stop=False)
+            for a in range(2):
+                nc.tensor.matmul_mx(out=z[:], lhsT=zt_w[:, a, fp4_cols].bitcast(FP4X4), lhsT_scale=w_scale(3 + a, m),
+                                    rhs=v2_w[c][:, a, :].bitcast(FP4X4), rhs_scale=v2_s[a][:, js],
+                                    start=False, stop=(a == 1))
+            th[i] = ring.tile([P, CHUNK], F32, name="th", bufs=8)
+            nc.scalar.activation(out=th[i][:], in_=z[:], func=ACT.Tanh, bias=half_b[:, m : m + 1], scale=0.5)
+
+        def subtract(i):
+            diff[i] = ring.tile([P, CHUNK], F32, name="diff", bufs=4)
+            nc.vector.tensor_tensor(out=diff[i][:], in0=av[i][:], in1=at[i][:], op=ALU.subtract)
+
+        def weigh(i):
+            gated[i] = ring.tile([P, CHUNK], F32, name="gated", bufs=3)
+            nc.vector.scalar_tensor_tensor(out=gated[i][:], in0=th[i][:], scalar=1.0, in1=diff[i][:], op0=ALU.add, op1=ALU.mult)
+
+        def finish(i, parts):
+            c, m, js, ns = place(i)
+            width = CHUNK // parts
+            for h in range(parts):
+                part = slice(h * width, (h + 1) * width)
+                res = ring.tile([P, width], F32, name="res", bufs=4)
+                nc.vector.scalar_tensor_tensor(out=res[:], in0=gated[i][:, part], scalar=0.5, in1=at[i][:, part], op0=ALU.mult, op1=ALU.add)
+                nc.sync.dma_start(out[ns, c * CHUNK + h * width : c * CHUNK + (h + 1) * width], res[:])
+
+        for i in range(MS):
+            text(i)
+        for i in range(2):
+            picture(i)
+            subtract(i)
+        for i in range(TILES - 1):
+            gate(i)
+            weigh(i)
+            if i + 2 < TILES:
+                if i + 2 >= MS:
+                    text(i + 2)
+                picture(i + 2)
+                subtract(i + 2)
+            else:
+                gate(i + 1)
+                weigh(i + 1)
+            finish(i, 1)
+        finish(TILES - 1, 2)

@@ -22,6 +22,7 @@ CHUNK = 512
 QUADS = 4
 MS = N // P
 TILES = MS * (J // CHUNK)
+HALF = N // 2
 
 
 def tile_list_gmu_silu_none_kernel(
@@ -41,7 +42,7 @@ def tile_list_gmu_silu_none_kernel(
         tab_s = keep.tile([P, T], U8, name="tab_s", align_bytes=64)
         tab2_s = keep.tile([P, T], U8, name="tab2_s", align_bytes=64)
         w_scales = keep.tile([P, 5 * N], U8, name="w_scales", align_bytes=64)
-        wt_w = keep.tile([P, 2, N], I32, name="wt_w", align_bytes=64)
+        wt_w = [keep.tile([P, 2, HALF], I32, name="wt_w%d" % h, align_bytes=64) for h in range(2)]
         zv_w = keep.tile([P, 2 * N], U8, name="zv_w", align_bytes=64)
         zt_w = keep.tile([P, 2, 2 * N], U8, name="zt_w", align_bytes=64)
         wv_raw = keep.tile([P, PACK, N], F32, name="wv_raw", align_bytes=64)
@@ -71,14 +72,15 @@ def tile_list_gmu_silu_none_kernel(
         cols = CHUNK // 16
         planes = w_scales[:].bitcast(I32).rearrange("p (a n) -> p a n", a=5)
         nc.sync.dma_start(list2[:], offs2)
-        with nc.allow_non_contiguous_dma(reason="one bias value for each partition"):
-            nc.sync.dma_start(b_sb[:], b.rearrange("(m p) -> p m", p=P))
+        nc.sync.dma_start(list1[:], offs)
         tab2_rows = tab2_scales.rearrange("a (q r) t -> r q a t", r=4).bitcast(I32)
         for r in range(4):
             nc.sync.dma_start(tab2_s[r:P:16, :].bitcast(I32), tab2_rows[r])
         nc.sync.dma_start(tab2_w[:], tab2_words[0].rearrange("p t i -> p (t i)").bitcast(I32))
-        nc.sync.dma_start(wt_w[:], wt_words.rearrange("a p n i -> p a (n i)").bitcast(I32))
-        nc.sync.dma_start(list1[:], offs)
+        wt_cols = wt_words.rearrange("a p n i -> p a (n i)").bitcast(I32)
+        nc.sync.dma_start(wt_w[0][:], wt_cols[:, :, 0:HALF])
+        with nc.allow_non_contiguous_dma(reason="one bias value for each partition"):
+            nc.sync.dma_start(b_sb[:], b.rearrange("(m p) -> p m", p=P))
         tab_rows = tab_scales[0].rearrange("(q r) t -> r q t", r=4).bitcast(I32)
         for r in range(4):
             nc.sync.dma_start(tab_s[r:P:32, :].bitcast(I32), tab_rows[r])
@@ -93,6 +95,7 @@ def tile_list_gmu_silu_none_kernel(
         nc.sync.dma_start(planes[0:16, 3:5, :], zt_scales.rearrange("a q n -> q a n").bitcast(I32))
         nc.sync.dma_start(zt_w[:].bitcast(I32), zt_words.rearrange("a p c -> p a c").bitcast(I32))
         nc.sync.dma_start(zv_w[:].bitcast(I32), zv_words[0].bitcast(I32))
+        nc.sync.dma_start(wt_w[1][:], wt_cols[:, :, HALF:N])
         for q in range(1, QUADS):
             nc.sync.dma_start(planes[32 * q : 32 * q + 4, 2:5, :], planes[4 * q : 4 * q + 4, 2:5, :])
 
@@ -115,7 +118,9 @@ def tile_list_gmu_silu_none_kernel(
         at, th, diff, gated = {}, {}, {}, {}
 
         def place(i):
-            c, m = divmod(i, MS)
+            h, rest = divmod(i, MS)
+            c, u = divmod(rest, 2)
+            m = 2 * h + u
             return c, m, slice(c * CHUNK, (c + 1) * CHUNK), slice(m * P, (m + 1) * P)
 
         def picture(i):
@@ -129,7 +134,7 @@ def tile_list_gmu_silu_none_kernel(
             c, m, js, ns = place(i)
             ht = psum.tile([P, CHUNK], F32, name="ht", tag="acc", bufs=8)
             for a in range(2):
-                nc.tensor.matmul_mx(out=ht[:], lhsT=wt_w[:, a, ns].bitcast(FP8X4), lhsT_scale=w_scale(a, m),
+                nc.tensor.matmul_mx(out=ht[:], lhsT=wt_w[m // 2][:, a, m % 2 * P : (m % 2 + 1) * P].bitcast(FP8X4), lhsT_scale=w_scale(a, m),
                                     rhs=v2_w[c][:, a, :].bitcast(FP4X4), rhs_scale=v2_s[a][:, js],
                                     start=(a == 0), stop=(a == 1))
             at[i] = ring.tile([P, CHUNK], F32, name="at", bufs=8)

@@ -45,7 +45,7 @@ def tile_list_gmu_silu_none_kernel(
         wt_w = [keep.tile([P, 2, HALF], I32, name="wt_w%d" % h, align_bytes=64) for h in range(2)]
         zv_w = keep.tile([P, 2 * N], U8, name="zv_w", align_bytes=64)
         zt_w = keep.tile([P, 2, 2 * N], U8, name="zt_w", align_bytes=64)
-        wv_raw = keep.tile([P, PACK, N], F32, name="wv_raw", align_bytes=64)
+        wv_raw = [keep.tile([P, PACK, HALF], F32, name="wv_raw%d" % h, align_bytes=64) for h in range(2)]
         wv_bf = keep.tile([P, N, PACK], BF16, name="wv_bf", align_bytes=64)
         wv_scales = keep.tile([P, N], U8, name="wv_scales", align_bytes=64)
         b_sb = keep.tile([P, MS], F32, name="b_sb")
@@ -78,13 +78,14 @@ def tile_list_gmu_silu_none_kernel(
             nc.sync.dma_start(tab2_s[r:P:16, :].bitcast(I32), tab2_rows[r])
         nc.sync.dma_start(tab2_w[:], tab2_words[0].rearrange("p t i -> p (t i)").bitcast(I32))
         wt_cols = wt_words.rearrange("a p n i -> p a (n i)").bitcast(I32)
-        nc.sync.dma_start(wt_w[0][:], wt_cols[:, :, 0:HALF])
         with nc.allow_non_contiguous_dma(reason="one bias value for each partition"):
             nc.sync.dma_start(b_sb[:], b.rearrange("(m p) -> p m", p=P))
         tab_rows = tab_scales[0].rearrange("(q r) t -> r q t", r=4).bitcast(I32)
         for r in range(4):
             nc.sync.dma_start(tab_s[r:P:32, :].bitcast(I32), tab_rows[r])
-        nc.sync.dma_start(wv_raw[:], wv.rearrange("(p i) n -> p i n", i=PACK))
+        for h in range(2):
+            nc.sync.dma_start(wv_raw[h][:], wv.rearrange("(p i) n -> p i n", i=PACK)[:, :, h * HALF : (h + 1) * HALF])
+        nc.sync.dma_start(wt_w[0][:], wt_cols[:, :, 0:HALF])
         nc.vector.tensor_copy(v2_s0[:], tab2_s[:].indirect(list2[:]))
         nc.sync.dma_start(v2_s1[0:112, :].bitcast(I32), v2_s0[16:P, :].bitcast(I32))
         wt_rows = wt_scales.rearrange("a (q r) n -> r q a n", r=4).bitcast(I32)
@@ -100,8 +101,9 @@ def tile_list_gmu_silu_none_kernel(
             nc.sync.dma_start(planes[32 * q : 32 * q + 4, 2:5, :], planes[4 * q : 4 * q + 4, 2:5, :])
 
         nc.scalar.mul(half_b[:], b_sb[:], 0.5)
-        nc.scalar.copy(out=wv_bf[:].rearrange("p (c i) t -> p c t i", i=4),
-                       in_=wv_raw[:].rearrange("p t (c i) -> p c t i", i=4))
+        for h in range(2):
+            nc.scalar.copy(out=wv_bf[:, h * HALF : (h + 1) * HALF, :].rearrange("p (c i) t -> p c t i", i=4),
+                           in_=wv_raw[h][:].rearrange("p t (c i) -> p c t i", i=4))
         for c in range(2):
             nc.vector.tensor_copy(pair[c][:], tab2_w[:].bitcast(U32).indirect(list2[:, c * cols : (c + 1) * cols]))
         for c in range(2):

@@ -172,6 +172,11 @@ def tile_list_gmu_silu_none_kernel(
                 nc.vector.scalar_tensor_tensor(out=res[:], in0=gated[i][:, part], scalar=0.5, in1=at[i][:, part], op0=ALU.mult, op1=ALU.add)
                 nc.sync.dma_start(out[ns, c * CHUNK + h * width : c * CHUNK + (h + 1) * width], res[:])
 
+        warm = psum.tile([P, CHUNK], F32, name="warm", tag="acc", bufs=8)
+        codes = pair[0][:].bitcast(U16)
+        for a in range(4):
+            nc.tensor.matmul_mx(out=warm[:], lhsT=codes[:, 0:P].bitcast(FP4X4), lhsT_scale=v2_s0[:, 0:P],
+                                rhs=codes[:, 0:CHUNK].bitcast(FP4X4), rhs_scale=v2_s0[:, 0:CHUNK], start=True, stop=True)
         for i in range(MS):
             text(i)
         for i in range(2):

@@ -45,8 +45,8 @@ def tile_list_gmu_silu_none_kernel(
         wt_w = [keep.tile([P, 2, HALF], I32, name="wt_w%d" % h, align_bytes=64) for h in range(2)]
         zv_w = keep.tile([P, 2 * N], U8, name="zv_w", align_bytes=64)
         zt_w = keep.tile([P, 2, 2 * N], U8, name="zt_w", align_bytes=64)
-        wv_raw = [keep.tile([P, PACK, HALF], F32, name="wv_raw%d" % h, align_bytes=64) for h in range(2)]
-        wv_bf = keep.tile([P, N, PACK], BF16, name="wv_bf", align_bytes=64)
+        wv_raw = [keep.tile([P, PACK, HALF], F32, name="wv_raw%d" % h, tag="raw%d" % h, align_bytes=64) for h in range(2)]
+        wv_bf = [keep.tile([P, HALF, PACK], BF16, name="wv_bf%d" % h, align_bytes=64) for h in range(2)]
         wv_scales = keep.tile([P, N], U8, name="wv_scales", align_bytes=64)
         b_sb = keep.tile([P, MS], F32, name="b_sb")
         half_b = keep.tile([P, MS], F32, name="half_b")
@@ -55,7 +55,6 @@ def tile_list_gmu_silu_none_kernel(
         v2_s1 = keep.tile([P, J], U8, name="v2_s1", align_bytes=64)
         v_w = [keep.tile([P, CHUNK], U32, name="v_w%d" % c, align_bytes=64) for c in range(2)]
         v2_w = [keep.tile([P, 2, CHUNK], U16, name="v2_w%d" % c, align_bytes=64) for c in range(2)]
-        av = [keep.tile([P, CHUNK], F32, name="av%d" % i) for i in range(TILES)]
 
         warm_in = keep.tile([P, 1], F32, name="warm_in")
         warm_out = keep.tile([P, 1], F32, name="warm_out")
@@ -83,8 +82,8 @@ def tile_list_gmu_silu_none_kernel(
         tab_rows = tab_scales[0].rearrange("(q r) t -> r q t", r=4).bitcast(I32)
         for r in range(4):
             nc.sync.dma_start(tab_s[r:P:32, :].bitcast(I32), tab_rows[r])
-        for h in range(2):
-            nc.sync.dma_start(wv_raw[h][:], wv.rearrange("(p i) n -> p i n", i=PACK)[:, :, h * HALF : (h + 1) * HALF])
+        wv_cols = wv.rearrange("(p i) n -> p i n", i=PACK)
+        nc.sync.dma_start(wv_raw[0][:], wv_cols[:, :, 0:HALF])
         nc.sync.dma_start(wt_w[0][:], wt_cols[:, :, 0:HALF])
         nc.vector.tensor_copy(v2_s0[:], tab2_s[:].indirect(list2[:]))
         nc.sync.dma_start(v2_s1[0:112, :].bitcast(I32), v2_s0[16:P, :].bitcast(I32))
@@ -94,30 +93,39 @@ def tile_list_gmu_silu_none_kernel(
         nc.sync.dma_start(tab_w[:], tab_words[0].rearrange("p t i -> p (t i)").bitcast(I32))
         nc.sync.dma_start(planes[0:16, 2:3, :], zv_scales.rearrange("a q n -> q a n").bitcast(I32))
         nc.sync.dma_start(planes[0:16, 3:5, :], zt_scales.rearrange("a q n -> q a n").bitcast(I32))
+        nc.sync.dma_start(wv_raw[1][:], wv_cols[:, :, HALF:N])
         nc.sync.dma_start(zt_w[:].bitcast(I32), zt_words.rearrange("a p c -> p a c").bitcast(I32))
         nc.sync.dma_start(zv_w[:].bitcast(I32), zv_words[0].bitcast(I32))
-        nc.sync.dma_start(wt_w[1][:], wt_cols[:, :, HALF:N])
         for q in range(1, QUADS):
             nc.sync.dma_start(planes[32 * q : 32 * q + 4, 2:5, :], planes[4 * q : 4 * q + 4, 2:5, :])
+        nc.sync.dma_start(wt_w[1][:], wt_cols[:, :, HALF:N])
 
         nc.scalar.mul(half_b[:], b_sb[:], 0.5)
         for h in range(2):
-            nc.scalar.copy(out=wv_bf[:, h * HALF : (h + 1) * HALF, :].rearrange("p (c i) t -> p c t i", i=4),
+            nc.scalar.copy(out=wv_bf[h][:].rearrange("p (c i) t -> p c t i", i=4),
                            in_=wv_raw[h][:].rearrange("p t (c i) -> p c t i", i=4))
         for c in range(2):
             nc.vector.tensor_copy(pair[c][:], tab2_w[:].bitcast(U32).indirect(list2[:, c * cols : (c + 1) * cols]))
         for c in range(2):
             nc.vector.tensor_copy(v2_w[c][:], pair[c][:].bitcast(U16).rearrange("p (j d) -> p d j", d=2))
         nc.vector.tensor_copy(v_s[:], tab_s[:].indirect(list1[:]))
-        nc.vector.quantize_mx(out=wv_codes[:].bitcast(FP8X4), scales=wv_scales[:], in_=wv_bf[:].rearrange("p n i -> p (n i)"))
+
+        def quantize(h):
+            ns = slice(h * HALF, (h + 1) * HALF)
+            nc.vector.quantize_mx(out=wv_codes[:, ns].bitcast(FP8X4), scales=wv_scales[:, ns], in_=wv_bf[h][:].rearrange("p n i -> p (n i)"))
+
+        quantize(0)
         for c in range(2):
             nc.vector.tensor_copy(v_w[c][:], tab_w[:].bitcast(U32).indirect(list1[:, c * cols : (c + 1) * cols]))
+        quantize(1)
         v2_s = [v2_s0, v2_s1]
 
         def w_scale(plane, m):
             return w_scales[:, plane * N + m * P : plane * N + (m + 1) * P]
 
         at, th, diff, gated = {}, {}, {}, {}
+        first_av = keep.tile([P, MS, CHUNK], F32, name="first_av", tag="raw1", align_bytes=64)
+        av = [first_av[:, i, :] if i < MS else keep.tile([P, CHUNK], F32, name="av%d" % i)[:] for i in range(TILES)]
 
         def place(i):
             h, rest = divmod(i, MS)
@@ -130,7 +138,7 @@ def tile_list_gmu_silu_none_kernel(
             hv = psum.tile([P, CHUNK], F32, name="hv", tag="acc", bufs=8)
             nc.tensor.matmul_mx(out=hv[:], lhsT=wv_codes[:, ns].bitcast(FP8X4), lhsT_scale=wv_scales[:, ns],
                                 rhs=v_w[c][:].bitcast(FP8X4), rhs_scale=v_s[:, js], start=True, stop=True)
-            nc.scalar.activation(out=av[i][:], in_=hv[:], func=ACT.Silu)
+            nc.scalar.activation(out=av[i], in_=hv[:], func=ACT.Silu)
 
         def text(i):
             c, m, js, ns = place(i)
@@ -157,7 +165,7 @@ def tile_list_gmu_silu_none_kernel(
 
         def subtract(i):
             diff[i] = ring.tile([P, CHUNK], F32, name="diff", bufs=4)
-            nc.vector.tensor_tensor(out=diff[i][:], in0=av[i][:], in1=at[i][:], op=ALU.subtract)
+            nc.vector.tensor_tensor(out=diff[i][:], in0=av[i], in1=at[i][:], op=ALU.subtract)
 
         def weigh(i):
             gated[i] = ring.tile([P, CHUNK], F32, name="gated", bufs=3)

@@ -72,11 +72,12 @@ def tile_list_gmu_silu_none_kernel(
         planes = w_scales[:].bitcast(I32).rearrange("p (a n) -> p a n", a=5)
         nc.sync.dma_start(list2[:], offs2)
         nc.sync.dma_start(list1[:], offs)
+        wt_cols = wt_words.rearrange("a p n i -> p a (n i)").bitcast(I32)
+        nc.sync.dma_start(wt_w[0][:], wt_cols[:, :, 0:HALF])
         tab2_rows = tab2_scales.rearrange("a (q r) t -> r q a t", r=4).bitcast(I32)
         for r in range(4):
             nc.sync.dma_start(tab2_s[r:P:16, :].bitcast(I32), tab2_rows[r])
         nc.sync.dma_start(tab2_w[:], tab2_words[0].rearrange("p t i -> p (t i)").bitcast(I32))
-        wt_cols = wt_words.rearrange("a p n i -> p a (n i)").bitcast(I32)
         with nc.allow_non_contiguous_dma(reason="one bias value for each partition"):
             nc.sync.dma_start(b_sb[:], b.rearrange("(m p) -> p m", p=P))
         tab_rows = tab_scales[0].rearrange("(q r) t -> r q t", r=4).bitcast(I32)
@@ -84,7 +85,6 @@ def tile_list_gmu_silu_none_kernel(
             nc.sync.dma_start(tab_s[r:P:32, :].bitcast(I32), tab_rows[r])
         wv_cols = wv.rearrange("(p i) n -> p i n", i=PACK)
         nc.sync.dma_start(wv_raw[0][:], wv_cols[:, :, 0:HALF])
-        nc.sync.dma_start(wt_w[0][:], wt_cols[:, :, 0:HALF])
         nc.vector.tensor_copy(v2_s0[:], tab2_s[:].indirect(list2[:]))
         nc.sync.dma_start(v2_s1[0:112, :].bitcast(I32), v2_s0[16:P, :].bitcast(I32))
         wt_rows = wt_scales.rearrange("a (q r) n -> r q a n", r=4).bitcast(I32)

@@ -1,6 +1,7 @@
 from contextlib import ExitStack
 
 import concourse.mybir as mybir
+from concourse.masks import make_identity
 
 K, L, N, T, J = 512, 1024, 512, 2048, 1024
 FLOPS = 2 * N * J * (2 * K + 2 * L)
@@ -23,6 +24,7 @@ QUADS = 4
 MS = N // P
 TILES = MS * (J // CHUNK)
 HALF = N // 2
+PIECE = CHUNK // 2
 
 
 def tile_list_gmu_silu_none_kernel(
@@ -58,10 +60,12 @@ def tile_list_gmu_silu_none_kernel(
 
         warm_in = keep.tile([P, 1], F32, name="warm_in")
         warm_out = keep.tile([P, 1], F32, name="warm_out")
-        pair = [keep.tile([P, CHUNK], U32, name="pair%d" % c, align_bytes=64) for c in range(2)]
+        pair = [keep.tile([P, PIECE], U32, name="pair%d" % g, align_bytes=64) for g in range(J // PIECE)]
         wv_codes = keep.tile([P, N], U32, name="wv_codes", align_bytes=64)
         nc.vector.memset(tab2_s[:, 0 : T // 2].bitcast(I32), 0)
         nc.gpsimd.memset(tab2_s[:, T // 2 : T].bitcast(I32), 0)
+        ident = keep.tile([P, P], F32, name="ident")
+        make_identity(nc, ident[:])
         nc.vector.memset(warm_in[:], 0.0)
         nc.scalar.activation(out=warm_out[:], in_=warm_in[:], func=ACT.Silu)
         nc.vector.memset(tab_s[:].bitcast(I32), 0)
@@ -72,24 +76,24 @@ def tile_list_gmu_silu_none_kernel(
         planes = w_scales[:].bitcast(I32).rearrange("p (a n) -> p a n", a=5)
         nc.sync.dma_start(list2[:], offs2)
         nc.sync.dma_start(list1[:], offs)
-        wt_cols = wt_words.rearrange("a p n i -> p a (n i)").bitcast(I32)
-        nc.sync.dma_start(wt_w[0][:], wt_cols[:, :, 0:HALF])
         tab2_rows = tab2_scales.rearrange("a (q r) t -> r q a t", r=4).bitcast(I32)
         for r in range(4):
             nc.sync.dma_start(tab2_s[r:P:16, :].bitcast(I32), tab2_rows[r])
         nc.sync.dma_start(tab2_w[:], tab2_words[0].rearrange("p t i -> p (t i)").bitcast(I32))
+        wt_cols = wt_words.rearrange("a p n i -> p a (n i)").bitcast(I32)
         with nc.allow_non_contiguous_dma(reason="one bias value for each partition"):
             nc.sync.dma_start(b_sb[:], b.rearrange("(m p) -> p m", p=P))
-        tab_rows = tab_scales[0].rearrange("(q r) t -> r q t", r=4).bitcast(I32)
-        for r in range(4):
-            nc.sync.dma_start(tab_s[r:P:32, :].bitcast(I32), tab_rows[r])
-        wv_cols = wv.rearrange("(p i) n -> p i n", i=PACK)
-        nc.sync.dma_start(wv_raw[0][:], wv_cols[:, :, 0:HALF])
-        nc.vector.tensor_copy(v2_s0[:], tab2_s[:].indirect(list2[:]))
-        nc.sync.dma_start(v2_s1[0:112, :].bitcast(I32), v2_s0[16:P, :].bitcast(I32))
         wt_rows = wt_scales.rearrange("a (q r) n -> r q a n", r=4).bitcast(I32)
         for r in range(4):
             nc.sync.dma_start(planes[r:P:32, 0:2, :], wt_rows[r])
+        wv_cols = wv.rearrange("(p i) n -> p i n", i=PACK)
+        nc.sync.dma_start(wt_w[0][:], wt_cols[:, :, 0:HALF])
+        nc.sync.dma_start(wv_raw[0][:], wv_cols[:, :, 0:HALF])
+        nc.vector.tensor_copy(v2_s0[:], tab2_s[:].indirect(list2[:]))
+        nc.sync.dma_start(v2_s1[0:112, :].bitcast(I32), v2_s0[16:P, :].bitcast(I32))
+        tab_rows = tab_scales[0].rearrange("(q r) t -> r q t", r=4).bitcast(I32)
+        for r in range(4):
+            nc.sync.dma_start(tab_s[r:P:32, :].bitcast(I32), tab_rows[r])
         nc.sync.dma_start(tab_w[:], tab_words[0].rearrange("p t i -> p (t i)").bitcast(I32))
         nc.sync.dma_start(planes[0:16, 2:3, :], zv_scales.rearrange("a q n -> q a n").bitcast(I32))
         nc.sync.dma_start(planes[0:16, 3:5, :], zt_scales.rearrange("a q n -> q a n").bitcast(I32))
@@ -101,13 +105,25 @@ def tile_list_gmu_silu_none_kernel(
         nc.sync.dma_start(wt_w[1][:], wt_cols[:, :, HALF:N])
 
         nc.scalar.mul(half_b[:], b_sb[:], 0.5)
-        for h in range(2):
+
+        def cast(h):
             nc.scalar.copy(out=wv_bf[h][:].rearrange("p (c i) t -> p c t i", i=4),
                            in_=wv_raw[h][:].rearrange("p t (c i) -> p c t i", i=4))
-        for c in range(2):
-            nc.vector.tensor_copy(pair[c][:], tab2_w[:].bitcast(U32).indirect(list2[:, c * cols : (c + 1) * cols]))
-        for c in range(2):
-            nc.vector.tensor_copy(v2_w[c][:], pair[c][:].bitcast(U16).rearrange("p (j d) -> p d j", d=2))
+
+        cast(0)
+
+        def gather_pairs(g):
+            nc.vector.tensor_copy(pair[g][:], tab2_w[:].bitcast(U32).indirect(list2[:, g * PIECE // 16 : (g + 1) * PIECE // 16]))
+
+        def part_pairs(g):
+            c, u = divmod(g, 2)
+            nc.vector.tensor_copy(v2_w[c][:, :, u * PIECE : (u + 1) * PIECE], pair[g][:].bitcast(U16).rearrange("p (j d) -> p d j", d=2))
+
+        gather_pairs(0)
+        for g in range(J // PIECE):
+            if g + 1 < J // PIECE:
+                gather_pairs(g + 1)
+            part_pairs(g)
         nc.vector.tensor_copy(v_s[:], tab_s[:].indirect(list1[:]))
 
         def quantize(h):
@@ -115,45 +131,51 @@ def tile_list_gmu_silu_none_kernel(
             nc.vector.quantize_mx(out=wv_codes[:, ns].bitcast(FP8X4), scales=wv_scales[:, ns], in_=wv_bf[h][:].rearrange("p n i -> p (n i)"))
 
         quantize(0)
-        for c in range(2):
+        for c in (1, 0):
             nc.vector.tensor_copy(v_w[c][:], tab_w[:].bitcast(U32).indirect(list1[:, c * cols : (c + 1) * cols]))
+        cast(1)
         quantize(1)
         v2_s = [v2_s0, v2_s1]
 
         def w_scale(plane, m):
             return w_scales[:, plane * N + m * P : plane * N + (m + 1) * P]
 
-        at, th, diff, gated = {}, {}, {}, {}
-        first_av = keep.tile([P, MS, CHUNK], F32, name="first_av", tag="raw1", align_bytes=64)
-        av = [first_av[:, i, :] if i < MS else keep.tile([P, CHUNK], F32, name="av%d" % i)[:] for i in range(TILES)]
+        av, at, th, diff, gated, minus_at = {}, {}, {}, {}, {}, {}
+
+        first_av = keep.tile([P, 2, CHUNK], F32, name="first_av", tag="raw1", align_bytes=64)
+
+        def bank(name, number):
+            return psum.tile([P, CHUNK], F32, name=name, tag="bank%d" % number)
 
         def place(i):
             h, rest = divmod(i, MS)
             c, u = divmod(rest, 2)
+            c = 1 - c
             m = 2 * h + u
             return c, m, slice(c * CHUNK, (c + 1) * CHUNK), slice(m * P, (m + 1) * P)
 
-        def picture(i):
+        def picture(i, number):
             c, m, js, ns = place(i)
-            hv = psum.tile([P, CHUNK], F32, name="hv", tag="acc", bufs=8)
+            hv = bank("hv", number)
             nc.tensor.matmul_mx(out=hv[:], lhsT=wv_codes[:, ns].bitcast(FP8X4), lhsT_scale=wv_scales[:, ns],
                                 rhs=v_w[c][:].bitcast(FP8X4), rhs_scale=v_s[:, js], start=True, stop=True)
+            av[i] = first_av[:, i, :] if i < 2 else ring.tile([P, CHUNK], F32, name="av", bufs=4)[:]
             nc.scalar.activation(out=av[i], in_=hv[:], func=ACT.Silu)
 
-        def text(i):
+        def text(i, number):
             c, m, js, ns = place(i)
-            ht = psum.tile([P, CHUNK], F32, name="ht", tag="acc", bufs=8)
+            ht = bank("ht", number)
             for a in range(2):
                 nc.tensor.matmul_mx(out=ht[:], lhsT=wt_w[m // 2][:, a, m % 2 * P : (m % 2 + 1) * P].bitcast(FP8X4), lhsT_scale=w_scale(a, m),
                                     rhs=v2_w[c][:, a, :].bitcast(FP4X4), rhs_scale=v2_s[a][:, js],
                                     start=(a == 0), stop=(a == 1))
-            at[i] = ring.tile([P, CHUNK], F32, name="at", bufs=8)
+            at[i] = ring.tile([P, CHUNK], F32, name="at", bufs=6)
             nc.scalar.activation(out=at[i][:], in_=ht[:], func=ACT.Silu)
 
-        def gate(i):
+        def gate(i, number):
             c, m, js, ns = place(i)
             fp4_cols = slice(2 * m * P, 2 * (m + 1) * P)
-            z = psum.tile([P, CHUNK], F32, name="z", tag="acc", bufs=8)
+            z = bank("z", number)
             nc.tensor.matmul_mx(out=z[:], lhsT=zv_w[:, fp4_cols].bitcast(FP4X4), lhsT_scale=w_scale(2, m),
                                 rhs=v_w[c][:].bitcast(FP8X4), rhs_scale=v_s[:, js], start=True, stop=False)
             for a in range(2):
@@ -163,43 +185,96 @@ def tile_list_gmu_silu_none_kernel(
             th[i] = ring.tile([P, CHUNK], F32, name="th", bufs=8)
             nc.scalar.activation(out=th[i][:], in_=z[:], func=ACT.Tanh, bias=half_b[:, m : m + 1], scale=0.5)
 
+        turned_nat, turned_av = {}, {}
+
+        def turned_text(k, number):
+            ht = bank("ht_turned", number)
+            for u in range(2):
+                jb = slice((2 * k + u) * P, (2 * k + u + 1) * P)
+                for a in range(2):
+                    nc.tensor.matmul_mx(out=ht[:, u * HALF : (u + 1) * HALF], lhsT=v2_w[0][:, a, jb].bitcast(FP4X4), lhsT_scale=v2_s[a][:, jb],
+                                        rhs=wt_w[0][:, a, :].bitcast(FP8X4), rhs_scale=w_scales[:, a * N : a * N + HALF],
+                                        start=(a == 0), stop=(a == 1))
+            plus = ring.tile([P, CHUNK], F32, name="turned_at", bufs=2)
+            nc.scalar.activation(out=plus[:], in_=ht[:], func=ACT.Silu)
+            turned_nat[k] = ring.tile([P, CHUNK], F32, name="turned_nat", bufs=2)
+            nc.scalar.mul(turned_nat[k][:], plus[:], -1.0)
+
+        def turned_picture(k, number):
+            hv = bank("hv_turned", number)
+            for u in range(2):
+                jb = slice((2 * k + u) * P, (2 * k + u + 1) * P)
+                nc.tensor.matmul_mx(out=hv[:, u * HALF : (u + 1) * HALF], lhsT=v_w[0][:, jb].bitcast(FP8X4), lhsT_scale=v_s[:, jb],
+                                    rhs=wv_codes[:, 0:HALF].bitcast(FP8X4), rhs_scale=wv_scales[:, 0:HALF], start=True, stop=True)
+            turned_av[k] = ring.tile([P, CHUNK], F32, name="turned_av", bufs=2)
+            nc.scalar.activation(out=turned_av[k][:], in_=hv[:], func=ACT.Silu)
+
+        def turn_back(dst, src, k, m, first, last):
+            for u in range(2):
+                nc.tensor.matmul(dst[:, (2 * k + u) * P : (2 * k + u + 1) * P], lhsT=src[:, u * HALF + m * P : u * HALF + (m + 1) * P], rhs=ident[:],
+                                 is_transpose=True, start=(first and u == 0), stop=(last and u == 1))
+
         def subtract(i):
             diff[i] = ring.tile([P, CHUNK], F32, name="diff", bufs=4)
             nc.vector.tensor_tensor(out=diff[i][:], in0=av[i], in1=at[i][:], op=ALU.subtract)
 
         def weigh(i):
-            gated[i] = ring.tile([P, CHUNK], F32, name="gated", bufs=3)
+            gated[i] = ring.tile([P, CHUNK], F32, name="gated", bufs=4)
             nc.vector.scalar_tensor_tensor(out=gated[i][:], in0=th[i][:], scalar=1.0, in1=diff[i][:], op0=ALU.add, op1=ALU.mult)
 
         def finish(i, parts):
             c, m, js, ns = place(i)
             width = CHUNK // parts
+            base, op = (minus_at[i], ALU.subtract) if i in minus_at else (at[i], ALU.add)
             for h in range(parts):
                 part = slice(h * width, (h + 1) * width)
                 res = ring.tile([P, width], F32, name="res", bufs=4)
-                nc.vector.scalar_tensor_tensor(out=res[:], in0=gated[i][:, part], scalar=0.5, in1=at[i][:, part], op0=ALU.mult, op1=ALU.add)
+                nc.vector.scalar_tensor_tensor(out=res[:], in0=gated[i][:, part], scalar=0.5, in1=base[:, part], op0=ALU.mult, op1=op)
                 nc.sync.dma_start(out[ns, c * CHUNK + h * width : c * CHUNK + (h + 1) * width], res[:])
 
-        warm = psum.tile([P, CHUNK], F32, name="warm", tag="acc", bufs=8)
+        warm = bank("warm", 7)
         codes = pair[0][:].bitcast(U16)
         for a in range(4):
             nc.tensor.matmul_mx(out=warm[:], lhsT=codes[:, 0:P].bitcast(FP4X4), lhsT_scale=v2_s0[:, 0:P],
-                                rhs=codes[:, 0:CHUNK].bitcast(FP4X4), rhs_scale=v2_s0[:, 0:CHUNK], start=True, stop=True)
-        for i in range(MS):
-            text(i)
+                                rhs=codes.bitcast(FP4X4), rhs_scale=v2_s0[:, 0:CHUNK], start=True, stop=True)
+        for k in range(2):
+            turned_text(k, k)
         for i in range(2):
-            picture(i)
-            subtract(i)
-        for i in range(TILES - 1):
-            gate(i)
+            text(i, i)
+        for m in range(2):
+            minus_at[2 + m] = bank("minus_at", 4 + m)
+            diff[2 + m] = bank("turned_diff", 6 + m)
+        for k in range(2):
+            for m in range(2):
+                turn_back(minus_at[2 + m], turned_nat[k], k, m, k == 0, k == 1)
+                turn_back(diff[2 + m], turned_nat[k], k, m, k == 0, False)
+        taken = []
+
+        def ring_bank():
+            taken.append(0)
+            return (len(taken) + 1) % 4
+
+        for first in (0, MS, MS + 2):
+            both = (first, first + 1)
+            for i in both:
+                if i >= MS:
+                    text(i, ring_bank())
+            for i in both:
+                picture(i, ring_bank())
+                subtract(i)
+            for i in both:
+                gate(i, ring_bank())
+                weigh(i)
+            for i in both:
+                finish(i, 1)
+        for k in range(2):
+            turned_picture(k, ring_bank())
+        for i in range(2, MS):
+            gate(i, ring_bank())
+        for m in range(2):
+            for k in range(2):
+                turn_back(diff[2 + m], turned_av[k], k, m, False, k == 1)
+        for i in range(2, MS):
             weigh(i)
-            if i + 2 < TILES:
-                if i + 2 >= MS:
-                    text(i + 2)
-                picture(i + 2)
-                subtract(i + 2)
-            else:
-                gate(i + 1)
-                weigh(i + 1)
-            finish(i, 1)
-        finish(TILES - 1, 2)
+        finish(2, 1)
+        finish(3, 2)

@@ -50,7 +50,7 @@ def tile_list_gmu_silu_none_kernel(
         wv_raw = [keep.tile([P, PACK, HALF], F32, name="wv_raw%d" % h, tag="raw%d" % h, align_bytes=64) for h in range(2)]
         wv_bf = [keep.tile([P, HALF, PACK], BF16, name="wv_bf%d" % h, align_bytes=64) for h in range(2)]
         wv_scales = keep.tile([P, N], U8, name="wv_scales", align_bytes=64)
-        b_sb = keep.tile([P, MS], F32, name="b_sb")
+        b_rows = keep.tile([P, P], F32, name="b_rows")
         half_b = keep.tile([P, MS], F32, name="half_b")
         v_s = keep.tile([P, J], U8, name="v_s", align_bytes=64)
         v2_s0 = keep.tile([P, J], U8, name="v2_s0", align_bytes=64)
@@ -68,6 +68,7 @@ def tile_list_gmu_silu_none_kernel(
         make_identity(nc, ident[:])
         nc.vector.memset(warm_in[:], 0.0)
         nc.scalar.activation(out=warm_out[:], in_=warm_in[:], func=ACT.Silu)
+        nc.vector.memset(b_rows[:], 0.0)
         nc.vector.memset(tab_s[:].bitcast(I32), 0)
         nc.vector.memset(w_scales[:].bitcast(I32), 0)
         nc.vector.memset(v2_s1[:].bitcast(I32), 0)
@@ -79,10 +80,9 @@ def tile_list_gmu_silu_none_kernel(
         tab2_rows = tab2_scales.rearrange("a (q r) t -> r q a t", r=4).bitcast(I32)
         for r in range(4):
             nc.sync.dma_start(tab2_s[r:P:16, :].bitcast(I32), tab2_rows[r])
+        nc.sync.dma_start(b_rows[0:MS, :], b.rearrange("(m p) -> m p", p=P))
         nc.sync.dma_start(tab2_w[:], tab2_words[0].rearrange("p t i -> p (t i)").bitcast(I32))
         wt_cols = wt_words.rearrange("a p n i -> p a (n i)").bitcast(I32)
-        with nc.allow_non_contiguous_dma(reason="one bias value for each partition"):
-            nc.sync.dma_start(b_sb[:], b.rearrange("(m p) -> p m", p=P))
         wt_rows = wt_scales.rearrange("a (q r) n -> r q a n", r=4).bitcast(I32)
         for r in range(4):
             nc.sync.dma_start(planes[r:P:32, 0:2, :], wt_rows[r])
@@ -104,7 +104,6 @@ def tile_list_gmu_silu_none_kernel(
             nc.sync.dma_start(planes[32 * q : 32 * q + 4, 2:5, :], planes[4 * q : 4 * q + 4, 2:5, :])
         nc.sync.dma_start(wt_w[1][:], wt_cols[:, :, HALF:N])
 
-        nc.scalar.mul(half_b[:], b_sb[:], 0.5)
 
         def cast(h):
             nc.scalar.copy(out=wv_bf[h][:].rearrange("p (c i) t -> p c t i", i=4),
@@ -232,6 +231,9 @@ def tile_list_gmu_silu_none_kernel(
                 nc.vector.scalar_tensor_tensor(out=res[:], in0=gated[i][:, part], scalar=0.5, in1=base[:, part], op0=ALU.mult, op1=op)
                 nc.sync.dma_start(out[ns, c * CHUNK + h * width : c * CHUNK + (h + 1) * width], res[:])
 
+        b_cols = bank("b_cols", 6)
+        nc.tensor.transpose(b_cols[:, 0:P], b_rows[:], ident[:])
+        nc.scalar.mul(half_b[:], b_cols[:, 0:MS], 0.5)
         warm = bank("warm", 7)
         codes = pair[0][:].bitcast(U16)
         for a in range(4):

@@ -45,8 +45,8 @@ def tile_list_gmu_silu_none_kernel(
         tab2_s = keep.tile([P, T], U8, name="tab2_s", align_bytes=64)
         w_scales = keep.tile([P, 5 * N], U8, name="w_scales", align_bytes=64)
         wt_w = [keep.tile([P, 2, HALF], I32, name="wt_w%d" % h, align_bytes=64) for h in range(2)]
-        zv_w = keep.tile([P, 2 * N], U8, name="zv_w", align_bytes=64)
-        zt_w = keep.tile([P, 2, 2 * N], U8, name="zt_w", align_bytes=64)
+        zv_w = [keep.tile([P, N], U8, name="zv_w%d" % h, align_bytes=64) for h in range(2)]
+        zt_w = [keep.tile([P, 2, N], U8, name="zt_w%d" % h, align_bytes=64) for h in range(2)]
         wv_raw = [keep.tile([P, PACK, HALF], F32, name="wv_raw%d" % h, tag="raw%d" % h, align_bytes=64) for h in range(2)]
         wv_bf = [keep.tile([P, HALF, PACK], BF16, name="wv_bf%d" % h, align_bytes=64) for h in range(2)]
         wv_scales = keep.tile([P, N], U8, name="wv_scales", align_bytes=64)
@@ -98,11 +98,16 @@ def tile_list_gmu_silu_none_kernel(
         nc.sync.dma_start(planes[0:16, 2:3, :], zv_scales.rearrange("a q n -> q a n").bitcast(I32))
         nc.sync.dma_start(planes[0:16, 3:5, :], zt_scales.rearrange("a q n -> q a n").bitcast(I32))
         nc.sync.dma_start(wv_raw[1][:], wv_cols[:, :, HALF:N])
-        nc.sync.dma_start(zt_w[:].bitcast(I32), zt_words.rearrange("a p c -> p a c").bitcast(I32))
-        nc.sync.dma_start(zv_w[:].bitcast(I32), zv_words[0].bitcast(I32))
+
+        def load_gate_words(h):
+            nc.sync.dma_start(zt_w[h][:].bitcast(I32), zt_words.rearrange("a p c -> p a c")[:, :, h * N : (h + 1) * N].bitcast(I32))
+            nc.sync.dma_start(zv_w[h][:].bitcast(I32), zv_words[0][:, h * N : (h + 1) * N].bitcast(I32))
+
+        load_gate_words(0)
         for q in range(1, QUADS):
             nc.sync.dma_start(planes[32 * q : 32 * q + 4, 2:5, :], planes[4 * q : 4 * q + 4, 2:5, :])
         nc.sync.dma_start(wt_w[1][:], wt_cols[:, :, HALF:N])
+        load_gate_words(1)
 
 
         def cast(h):
@@ -173,12 +178,12 @@ def tile_list_gmu_silu_none_kernel(
 
         def gate(i, number):
             c, m, js, ns = place(i)
-            fp4_cols = slice(2 * m * P, 2 * (m + 1) * P)
+            fp4_cols = slice(2 * (m % 2) * P, 2 * (m % 2 + 1) * P)
             z = bank("z", number)
-            nc.tensor.matmul_mx(out=z[:], lhsT=zv_w[:, fp4_cols].bitcast(FP4X4), lhsT_scale=w_scale(2, m),
+            nc.tensor.matmul_mx(out=z[:], lhsT=zv_w[m // 2][:, fp4_cols].bitcast(FP4X4), lhsT_scale=w_scale(2, m),
                                 rhs=v_w[c][:].bitcast(FP8X4), rhs_scale=v_s[:, js], start=True, stop=False)
             for a in range(2):
-                nc.tensor.matmul_mx(out=z[:], lhsT=zt_w[:, a, fp4_cols].bitcast(FP4X4), lhsT_scale=w_scale(3 + a, m),
+                nc.tensor.matmul_mx(out=z[:], lhsT=zt_w[m // 2][:, a, fp4_cols].bitcast(FP4X4), lhsT_scale=w_scale(3 + a, m),
                                     rhs=v2_w[c][:, a, :].bitcast(FP4X4), rhs_scale=v2_s[a][:, js],
                                     start=False, stop=(a == 1))
             th[i] = ring.tile([P, CHUNK], F32, name="th", bufs=8)

@@ -89,11 +89,11 @@ def tile_list_gmu_silu_none_kernel(
         wv_cols = wv.rearrange("(p i) n -> p i n", i=PACK)
         nc.sync.dma_start(wt_w[0][:], wt_cols[:, :, 0:HALF])
         nc.sync.dma_start(wv_raw[0][:], wv_cols[:, :, 0:HALF])
-        nc.vector.tensor_copy(v2_s0[:], tab2_s[:].indirect(list2[:]))
-        nc.sync.dma_start(v2_s1[0:112, :].bitcast(I32), v2_s0[16:P, :].bitcast(I32))
         tab_rows = tab_scales[0].rearrange("(q r) t -> r q t", r=4).bitcast(I32)
         for r in range(4):
             nc.sync.dma_start(tab_s[r:P:32, :].bitcast(I32), tab_rows[r])
+        nc.vector.tensor_copy(v2_s0[:], tab2_s[:].indirect(list2[:]))
+        nc.sync.dma_start(v2_s1[0:112, :].bitcast(I32), v2_s0[16:P, :].bitcast(I32))
         nc.sync.dma_start(tab_w[:], tab_words[0].rearrange("p t i -> p (t i)").bitcast(I32))
         nc.sync.dma_start(planes[0:16, 2:3, :], zv_scales.rearrange("a q n -> q a n").bitcast(I32))
         nc.sync.dma_start(planes[0:16, 3:5, :], zt_scales.rearrange("a q n -> q a n").bitcast(I32))

@@ -53,8 +53,8 @@ def tile_list_gmu_silu_none_kernel(
         b_rows = keep.tile([P, P], F32, name="b_rows")
         half_b = keep.tile([P, MS], F32, name="half_b")
         v_s = keep.tile([P, J], U8, name="v_s", align_bytes=64)
-        v2_s0 = keep.tile([P, J], U8, name="v2_s0", align_bytes=64)
-        v2_s1 = keep.tile([P, J], U8, name="v2_s1", align_bytes=64)
+        v2_rows = keep.tile([P, J], U8, name="v2_rows", align_bytes=64)
+        v2_planes = keep.tile([P, 2 * J], U8, name="v2_planes", align_bytes=64)
         v_w = [keep.tile([P, CHUNK], U32, name="v_w%d" % c, align_bytes=64) for c in range(2)]
         v2_w = [keep.tile([P, 2, CHUNK], U16, name="v2_w%d" % c, align_bytes=64) for c in range(2)]
 
@@ -62,25 +62,21 @@ def tile_list_gmu_silu_none_kernel(
         warm_out = keep.tile([P, 1], F32, name="warm_out")
         pair = [keep.tile([P, PIECE], U32, name="pair%d" % g, align_bytes=64) for g in range(J // PIECE)]
         wv_codes = keep.tile([P, N], U32, name="wv_codes", align_bytes=64)
-        nc.vector.memset(tab2_s[:, 0 : T // 2].bitcast(I32), 0)
-        nc.gpsimd.memset(tab2_s[:, T // 2 : T].bitcast(I32), 0)
+        nc.vector.memset(w_scales[:].bitcast(I32), 0)
+        nc.gpsimd.memset(tab2_s[0:96, :].bitcast(I32), 0)
         ident = keep.tile([P, P], F32, name="ident")
         make_identity(nc, ident[:])
         nc.vector.memset(warm_in[:], 0.0)
         nc.scalar.activation(out=warm_out[:], in_=warm_in[:], func=ACT.Silu)
         nc.vector.memset(b_rows[:], 0.0)
         nc.vector.memset(tab_s[:].bitcast(I32), 0)
-        nc.vector.memset(w_scales[:].bitcast(I32), 0)
-        nc.vector.memset(v2_s1[:].bitcast(I32), 0)
+        nc.vector.memset(v2_planes[:].bitcast(I32), 0)
 
         cols = CHUNK // 16
         planes = w_scales[:].bitcast(I32).rearrange("p (a n) -> p a n", a=5)
         nc.sync.dma_start(list2[:], offs2)
+        nc.sync.dma_start(tab2_s[96:P, :].bitcast(I32), tab2_scales.rearrange("a q t -> q a t").bitcast(I32))
         nc.sync.dma_start(list1[:], offs)
-        tab2_rows = tab2_scales.rearrange("a (q r) t -> r q a t", r=4).bitcast(I32)
-        for r in range(4):
-            nc.sync.dma_start(tab2_s[r:P:16, :].bitcast(I32), tab2_rows[r])
-        nc.sync.dma_start(b_rows[0:MS, :], b.rearrange("(m p) -> m p", p=P))
         nc.sync.dma_start(tab2_w[:], tab2_words[0].rearrange("p t i -> p (t i)").bitcast(I32))
         wt_cols = wt_words.rearrange("a p n i -> p a (n i)").bitcast(I32)
         wt_rows = wt_scales.rearrange("a (q r) n -> r q a n", r=4).bitcast(I32)
@@ -89,11 +85,14 @@ def tile_list_gmu_silu_none_kernel(
         wv_cols = wv.rearrange("(p i) n -> p i n", i=PACK)
         nc.sync.dma_start(wt_w[0][:], wt_cols[:, :, 0:HALF])
         nc.sync.dma_start(wv_raw[0][:], wv_cols[:, :, 0:HALF])
+        nc.sync.dma_start(b_rows[0:MS, :], b.rearrange("(m p) -> m p", p=P))
+        nc.vector.tensor_copy(v2_rows[:], tab2_s[:].indirect(list2[:]))
+        both_planes = v2_planes[:].bitcast(I32).rearrange("p (a j) -> p a j", a=2)
+        for q in range(QUADS):
+            nc.sync.dma_start(both_planes[32 * q : 32 * q + 4], v2_rows[96 + 8 * q : 96 + 8 * (q + 1), :].bitcast(I32))
         tab_rows = tab_scales[0].rearrange("(q r) t -> r q t", r=4).bitcast(I32)
         for r in range(4):
             nc.sync.dma_start(tab_s[r:P:32, :].bitcast(I32), tab_rows[r])
-        nc.vector.tensor_copy(v2_s0[:], tab2_s[:].indirect(list2[:]))
-        nc.sync.dma_start(v2_s1[0:112, :].bitcast(I32), v2_s0[16:P, :].bitcast(I32))
         nc.sync.dma_start(tab_w[:], tab_words[0].rearrange("p t i -> p (t i)").bitcast(I32))
         nc.sync.dma_start(planes[0:16, 2:3, :], zv_scales.rearrange("a q n -> q a n").bitcast(I32))
         nc.sync.dma_start(planes[0:16, 3:5, :], zt_scales.rearrange("a q n -> q a n").bitcast(I32))
@@ -139,7 +138,7 @@ def tile_list_gmu_silu_none_kernel(
             nc.vector.tensor_copy(v_w[c][:], tab_w[:].bitcast(U32).indirect(list1[:, c * cols : (c + 1) * cols]))
         cast(1)
         quantize(1)
-        v2_s = [v2_s0, v2_s1]
+        v2_s = [v2_planes[:, a * J : (a + 1) * J] for a in range(2)]
 
         def w_scale(plane, m):
             return w_scales[:, plane * N + m * P : plane * N + (m + 1) * P]
@@ -242,8 +241,8 @@ def tile_list_gmu_silu_none_kernel(
         warm = bank("warm", 7)
         codes = pair[0][:].bitcast(U16)
         for a in range(4):
-            nc.tensor.matmul_mx(out=warm[:], lhsT=codes[:, 0:P].bitcast(FP4X4), lhsT_scale=v2_s0[:, 0:P],
-                                rhs=codes.bitcast(FP4X4), rhs_scale=v2_s0[:, 0:CHUNK], start=True, stop=True)
+            nc.tensor.matmul_mx(out=warm[:], lhsT=codes[:, 0:P].bitcast(FP4X4), lhsT_scale=v2_rows[:, 0:P],
+                                rhs=codes.bitcast(FP4X4), rhs_scale=v2_rows[:, 0:CHUNK], start=True, stop=True)
         for k in range(2):
             turned_text(k, k)
         for i in range(2):

@@ -238,11 +238,6 @@ def tile_list_gmu_silu_none_kernel(
         b_cols = bank("b_cols", 6)
         nc.tensor.transpose(b_cols[:, 0:P], b_rows[:], ident[:])
         nc.scalar.mul(half_b[:], b_cols[:, 0:MS], 0.5)
-        warm = bank("warm", 7)
-        codes = pair[0][:].bitcast(U16)
-        for a in range(4):
-            nc.tensor.matmul_mx(out=warm[:], lhsT=codes[:, 0:P].bitcast(FP4X4), lhsT_scale=v2_rows[:, 0:P],
-                                rhs=codes.bitcast(FP4X4), rhs_scale=v2_rows[:, 0:CHUNK], start=True, stop=True)
         for k in range(2):
             turned_text(k, k)
         for i in range(2):

from contextlib import ExitStack

import concourse.mybir as mybir
from concourse.masks import make_identity

K, L, N, T, J = 512, 1024, 512, 2048, 1024
FLOPS = 2 * N * J * (2 * K + 2 * L)

F32 = mybir.dt.float32
BF16 = mybir.dt.bfloat16
I32 = mybir.dt.int32
U32 = mybir.dt.uint32
U16 = mybir.dt.uint16
U8 = mybir.dt.uint8
FP8X4 = mybir.dt.float8_e4m3fn_x4
FP4X4 = mybir.dt.float4_e2m1fn_x4
ALU = mybir.AluOpType
ACT = mybir.ActivationFunctionType

P = 128
PACK = 4
CHUNK = 512
QUADS = 4
MS = N // P
TILES = MS * (J // CHUNK)
HALF = N // 2
PIECE = CHUNK // 2


def tile_list_gmu_silu_none_kernel(
    tc, tab_words, tab_scales, tab2_words, tab2_scales, zv_words, zv_scales, zt_words, zt_scales,
    b, wv, wt_words, wt_scales, offs, offs2, out,
):
    nc = tc.nc
    with ExitStack() as ctx:
        keep = ctx.enter_context(tc.tile_pool(name="keep", bufs=1))
        ring = ctx.enter_context(tc.tile_pool(name="ring", bufs=3))
        psum = ctx.enter_context(tc.psum_pool(name="psum", bufs=1))

        list1 = keep.tile([P, J // 16], U16, name="list1")
        list2 = keep.tile([P, J // 16], U16, name="list2")
        tab_w = keep.tile([P, T], I32, name="tab_w", align_bytes=64)
        tab2_w = keep.tile([P, T], I32, name="tab2_w", align_bytes=64)
        tab_s = keep.tile([P, T], U8, name="tab_s", align_bytes=64)
        tab2_s = keep.tile([P, T], U8, name="tab2_s", align_bytes=64)
        w_scales = keep.tile([P, 5 * N], U8, name="w_scales", align_bytes=64)
        wt_w = [keep.tile([P, 2, HALF], I32, name="wt_w%d" % h, align_bytes=64) for h in range(2)]
        zv_w = [keep.tile([P, N], U8, name="zv_w%d" % h, align_bytes=64) for h in range(2)]
        zt_w = [keep.tile([P, 2, N], U8, name="zt_w%d" % h, align_bytes=64) for h in range(2)]
        wv_raw = [keep.tile([P, PACK, HALF], F32, name="wv_raw%d" % h, tag="raw%d" % h, align_bytes=64) for h in range(2)]
        wv_bf = [keep.tile([P, HALF, PACK], BF16, name="wv_bf%d" % h, align_bytes=64) for h in range(2)]
        wv_scales = keep.tile([P, N], U8, name="wv_scales", align_bytes=64)
        b_rows = keep.tile([P, P], F32, name="b_rows")
        half_b = keep.tile([P, MS], F32, name="half_b")
        v_s = keep.tile([P, J], U8, name="v_s", align_bytes=64)
        v2_rows = keep.tile([P, J], U8, name="v2_rows", align_bytes=64)
        v2_planes = keep.tile([P, 2 * J], U8, name="v2_planes", align_bytes=64)
        v_w = [keep.tile([P, CHUNK], U32, name="v_w%d" % c, align_bytes=64) for c in range(2)]
        v2_w = [keep.tile([P, 2, CHUNK], U16, name="v2_w%d" % c, align_bytes=64) for c in range(2)]

        warm_in = keep.tile([P, 1], F32, name="warm_in")
        warm_out = keep.tile([P, 1], F32, name="warm_out")
        pair = [keep.tile([P, PIECE], U32, name="pair%d" % g, align_bytes=64) for g in range(J // PIECE)]
        wv_codes = keep.tile([P, N], U32, name="wv_codes", align_bytes=64)
        nc.vector.memset(w_scales[:].bitcast(I32), 0)
        nc.gpsimd.memset(tab2_s[0:96, :].bitcast(I32), 0)
        ident = keep.tile([P, P], F32, name="ident")
        make_identity(nc, ident[:])
        nc.vector.memset(warm_in[:], 0.0)
        nc.scalar.activation(out=warm_out[:], in_=warm_in[:], func=ACT.Silu)
        nc.vector.memset(b_rows[:], 0.0)
        nc.vector.memset(tab_s[:].bitcast(I32), 0)
        nc.vector.memset(v2_planes[:].bitcast(I32), 0)

        cols = CHUNK // 16
        planes = w_scales[:].bitcast(I32).rearrange("p (a n) -> p a n", a=5)
        nc.sync.dma_start(list2[:], offs2)
        nc.sync.dma_start(tab2_s[96:P, :].bitcast(I32), tab2_scales.rearrange("a q t -> q a t").bitcast(I32))
        nc.sync.dma_start(list1[:], offs)
        nc.sync.dma_start(tab2_w[:], tab2_words[0].rearrange("p t i -> p (t i)").bitcast(I32))
        wt_cols = wt_words.rearrange("a p n i -> p a (n i)").bitcast(I32)
        wt_rows = wt_scales.rearrange("a (q r) n -> r q a n", r=4).bitcast(I32)
        for r in range(4):
            nc.sync.dma_start(planes[r:P:32, 0:2, :], wt_rows[r])
        wv_cols = wv.rearrange("(p i) n -> p i n", i=PACK)
        nc.sync.dma_start(wt_w[0][:], wt_cols[:, :, 0:HALF])
        nc.sync.dma_start(wv_raw[0][:], wv_cols[:, :, 0:HALF])
        nc.sync.dma_start(b_rows[0:MS, :], b.rearrange("(m p) -> m p", p=P))
        nc.vector.tensor_copy(v2_rows[:], tab2_s[:].indirect(list2[:]))
        both_planes = v2_planes[:].bitcast(I32).rearrange("p (a j) -> p a j", a=2)
        for q in range(QUADS):
            nc.sync.dma_start(both_planes[32 * q : 32 * q + 4], v2_rows[96 + 8 * q : 96 + 8 * (q + 1), :].bitcast(I32))
        tab_rows = tab_scales[0].rearrange("(q r) t -> r q t", r=4).bitcast(I32)
        for r in range(4):
            nc.sync.dma_start(tab_s[r:P:32, :].bitcast(I32), tab_rows[r])
        nc.sync.dma_start(tab_w[:], tab_words[0].rearrange("p t i -> p (t i)").bitcast(I32))
        nc.sync.dma_start(planes[0:16, 2:3, :], zv_scales.rearrange("a q n -> q a n").bitcast(I32))
        nc.sync.dma_start(planes[0:16, 3:5, :], zt_scales.rearrange("a q n -> q a n").bitcast(I32))
        nc.sync.dma_start(wv_raw[1][:], wv_cols[:, :, HALF:N])

        def load_gate_words(h):
            nc.sync.dma_start(zt_w[h][:].bitcast(I32), zt_words.rearrange("a p c -> p a c")[:, :, h * N : (h + 1) * N].bitcast(I32))
            nc.sync.dma_start(zv_w[h][:].bitcast(I32), zv_words[0][:, h * N : (h + 1) * N].bitcast(I32))

        load_gate_words(0)
        for q in range(1, QUADS):
            nc.sync.dma_start(planes[32 * q : 32 * q + 4, 2:5, :], planes[4 * q : 4 * q + 4, 2:5, :])
        nc.sync.dma_start(wt_w[1][:], wt_cols[:, :, HALF:N])
        load_gate_words(1)


        def cast(h):
            nc.scalar.copy(out=wv_bf[h][:].rearrange("p (c i) t -> p c t i", i=4),
                           in_=wv_raw[h][:].rearrange("p t (c i) -> p c t i", i=4))

        cast(0)

        def gather_pairs(g):
            nc.vector.tensor_copy(pair[g][:], tab2_w[:].bitcast(U32).indirect(list2[:, g * PIECE // 16 : (g + 1) * PIECE // 16]))

        def part_pairs(g):
            c, u = divmod(g, 2)
            nc.vector.tensor_copy(v2_w[c][:, :, u * PIECE : (u + 1) * PIECE], pair[g][:].bitcast(U16).rearrange("p (j d) -> p d j", d=2))

        gather_pairs(0)
        for g in range(J // PIECE):
            if g + 1 < J // PIECE:
                gather_pairs(g + 1)
            part_pairs(g)
        nc.vector.tensor_copy(v_s[:], tab_s[:].indirect(list1[:]))

        def quantize(h):
            ns = slice(h * HALF, (h + 1) * HALF)
            nc.vector.quantize_mx(out=wv_codes[:, ns].bitcast(FP8X4), scales=wv_scales[:, ns], in_=wv_bf[h][:].rearrange("p n i -> p (n i)"))

        quantize(0)
        for c in (1, 0):
            nc.vector.tensor_copy(v_w[c][:], tab_w[:].bitcast(U32).indirect(list1[:, c * cols : (c + 1) * cols]))
        cast(1)
        quantize(1)
        v2_s = [v2_planes[:, a * J : (a + 1) * J] for a in range(2)]

        def w_scale(plane, m):
            return w_scales[:, plane * N + m * P : plane * N + (m + 1) * P]

        av, at, th, diff, gated, minus_at = {}, {}, {}, {}, {}, {}

        first_av = keep.tile([P, 2, CHUNK], F32, name="first_av", tag="raw1", align_bytes=64)

        def bank(name, number):
            return psum.tile([P, CHUNK], F32, name=name, tag="bank%d" % number)

        def place(i):
            h, rest = divmod(i, MS)
            c, u = divmod(rest, 2)
            c = 1 - c
            m = 2 * h + u
            return c, m, slice(c * CHUNK, (c + 1) * CHUNK), slice(m * P, (m + 1) * P)

        def picture(i, number):
            c, m, js, ns = place(i)
            hv = bank("hv", number)
            nc.tensor.matmul_mx(out=hv[:], lhsT=wv_codes[:, ns].bitcast(FP8X4), lhsT_scale=wv_scales[:, ns],
                                rhs=v_w[c][:].bitcast(FP8X4), rhs_scale=v_s[:, js], start=True, stop=True)
            av[i] = first_av[:, i, :] if i < 2 else ring.tile([P, CHUNK], F32, name="av", bufs=4)[:]
            nc.scalar.activation(out=av[i], in_=hv[:], func=ACT.Silu)

        def text(i, number):
            c, m, js, ns = place(i)
            ht = bank("ht", number)
            for a in range(2):
                nc.tensor.matmul_mx(out=ht[:], lhsT=wt_w[m // 2][:, a, m % 2 * P : (m % 2 + 1) * P].bitcast(FP8X4), lhsT_scale=w_scale(a, m),
                                    rhs=v2_w[c][:, a, :].bitcast(FP4X4), rhs_scale=v2_s[a][:, js],
                                    start=(a == 0), stop=(a == 1))
            at[i] = ring.tile([P, CHUNK], F32, name="at", bufs=6)
            nc.scalar.activation(out=at[i][:], in_=ht[:], func=ACT.Silu)

        def gate(i, number):
            c, m, js, ns = place(i)
            fp4_cols = slice(2 * (m % 2) * P, 2 * (m % 2 + 1) * P)
            z = bank("z", number)
            nc.tensor.matmul_mx(out=z[:], lhsT=zv_w[m // 2][:, fp4_cols].bitcast(FP4X4), lhsT_scale=w_scale(2, m),
                                rhs=v_w[c][:].bitcast(FP8X4), rhs_scale=v_s[:, js], start=True, stop=False)
            for a in range(2):
                nc.tensor.matmul_mx(out=z[:], lhsT=zt_w[m // 2][:, a, fp4_cols].bitcast(FP4X4), lhsT_scale=w_scale(3 + a, m),
                                    rhs=v2_w[c][:, a, :].bitcast(FP4X4), rhs_scale=v2_s[a][:, js],
                                    start=False, stop=(a == 1))
            th[i] = ring.tile([P, CHUNK], F32, name="th", bufs=8)
            nc.scalar.activation(out=th[i][:], in_=z[:], func=ACT.Tanh, bias=half_b[:, m : m + 1], scale=0.5)

        turned_nat, turned_av = {}, {}

        def turned_text(k, number):
            ht = bank("ht_turned", number)
            for u in range(2):
                jb = slice((2 * k + u) * P, (2 * k + u + 1) * P)
                for a in range(2):
                    nc.tensor.matmul_mx(out=ht[:, u * HALF : (u + 1) * HALF], lhsT=v2_w[0][:, a, jb].bitcast(FP4X4), lhsT_scale=v2_s[a][:, jb],
                                        rhs=wt_w[0][:, a, :].bitcast(FP8X4), rhs_scale=w_scales[:, a * N : a * N + HALF],
                                        start=(a == 0), stop=(a == 1))
            plus = ring.tile([P, CHUNK], F32, name="turned_at", bufs=2)
            nc.scalar.activation(out=plus[:], in_=ht[:], func=ACT.Silu)
            turned_nat[k] = ring.tile([P, CHUNK], F32, name="turned_nat", bufs=2)
            nc.scalar.mul(turned_nat[k][:], plus[:], -1.0)

        def turned_picture(k, number):
            hv = bank("hv_turned", number)
            for u in range(2):
                jb = slice((2 * k + u) * P, (2 * k + u + 1) * P)
                nc.tensor.matmul_mx(out=hv[:, u * HALF : (u + 1) * HALF], lhsT=v_w[0][:, jb].bitcast(FP8X4), lhsT_scale=v_s[:, jb],
                                    rhs=wv_codes[:, 0:HALF].bitcast(FP8X4), rhs_scale=wv_scales[:, 0:HALF], start=True, stop=True)
            turned_av[k] = ring.tile([P, CHUNK], F32, name="turned_av", bufs=2)
            nc.scalar.activation(out=turned_av[k][:], in_=hv[:], func=ACT.Silu)

        def turn_back(dst, src, k, m, first, last):
            for u in range(2):
                nc.tensor.matmul(dst[:, (2 * k + u) * P : (2 * k + u + 1) * P], lhsT=src[:, u * HALF + m * P : u * HALF + (m + 1) * P], rhs=ident[:],
                                 is_transpose=True, start=(first and u == 0), stop=(last and u == 1))

        def subtract(i):
            diff[i] = ring.tile([P, CHUNK], F32, name="diff", bufs=4)
            nc.vector.tensor_tensor(out=diff[i][:], in0=av[i], in1=at[i][:], op=ALU.subtract)

        def weigh(i):
            gated[i] = ring.tile([P, CHUNK], F32, name="gated", bufs=4)
            nc.vector.scalar_tensor_tensor(out=gated[i][:], in0=th[i][:], scalar=1.0, in1=diff[i][:], op0=ALU.add, op1=ALU.mult)

        def finish(i, parts):
            c, m, js, ns = place(i)
            width = CHUNK // parts
            base, op = (minus_at[i], ALU.subtract) if i in minus_at else (at[i], ALU.add)
            for h in range(parts):
                part = slice(h * width, (h + 1) * width)
                res = ring.tile([P, width], F32, name="res", bufs=4)
                nc.vector.scalar_tensor_tensor(out=res[:], in0=gated[i][:, part], scalar=0.5, in1=base[:, part], op0=ALU.mult, op1=op)
                nc.sync.dma_start(out[ns, c * CHUNK + h * width : c * CHUNK + (h + 1) * width], res[:])

        b_cols = bank("b_cols", 6)
        nc.tensor.transpose(b_cols[:, 0:P], b_rows[:], ident[:])
        nc.scalar.mul(half_b[:], b_cols[:, 0:MS], 0.5)
        for k in range(2):
            turned_text(k, k)
        for i in range(2):
            text(i, i)
        for m in range(2):
            minus_at[2 + m] = bank("minus_at", 4 + m)
            diff[2 + m] = bank("turned_diff", 6 + m)
        for k in range(2):
            for m in range(2):
                turn_back(minus_at[2 + m], turned_nat[k], k, m, k == 0, k == 1)
                turn_back(diff[2 + m], turned_nat[k], k, m, k == 0, False)
        taken = []

        def ring_bank():
            taken.append(0)
            return (len(taken) + 1) % 4

        for first in (0, MS, MS + 2):
            both = (first, first + 1)
            for i in both:
                if i >= MS:
                    text(i, ring_bank())
            for i in both:
                picture(i, ring_bank())
                subtract(i)
            for i in both:
                gate(i, ring_bank())
                weigh(i)
            for i in both:
                finish(i, 1)
        for k in range(2):
            turned_picture(k, ring_bank())
        for i in range(2, MS):
            gate(i, ring_bank())
        for m in range(2):
            for k in range(2):
                turn_back(diff[2 + m], turned_av[k], k, m, False, k == 1)
        for i in range(2, MS):
            weigh(i)
        finish(2, 1)
        finish(3, 2)
